import numpy as np, ml_dtypes
CORES = [3,11,19,27,35,43,51,59]
N = 8
BF = ml_dtypes.bfloat16
def gentries(a):
    return np.ascontiguousarray(a.reshape(8, 16, -1).transpose(0, 2, 1)).reshape(8, -1)
def gtable(e):
    e = np.asarray(e); return np.ascontiguousarray(e.reshape(8, -1, 16).transpose(0, 2, 1)).reshape(128, -1).astype(np.int32)
S, P, CAP, R = 8192, 1024, 288, 5
LEAST = -(-P // CAP)
def counts(rng, m):
    w = np.repeat(np.exp2(rng.integers(-2, 3, m)), CAP - 1); slot = np.argsort(-rng.random(m * (CAP - 1)) * w)[:P - m] // (CAP - 1)
    return np.bincount(slot, minlength=R) + (np.arange(R) < m)
def fountain(rng, cnt, src, e=1, full=False):
    pk = np.zeros((N, 128, P), np.float32); nb = np.zeros((N, 8, 4, P), np.int64)
    def pick(n):
        return np.minimum((rng.random(S) ** e * n).astype(np.int64), n - 1)
    for g in range(8):
        rd = np.concatenate([rng.permutation(np.repeat(np.arange(R), cnt[q, g])) for q in range(N)])
        at = np.argsort(rd, kind="stable"); t = rd[at]; end = np.concatenate([[0], np.cumsum(np.bincount(rd, minlength=R))])
        hi = end[t]; lo = end[np.maximum(t - 1, 0)]; most = np.maximum(hi, 3)
        a = lo + pick(np.maximum(hi - lo, 1))
        b = pick(most - 1); b = b + (b >= a)
        c = pick(most - 2); c = c + (c >= np.minimum(a, b)); c = c + (c >= np.maximum(a, b))
        if e > 1:
            o = np.concatenate([[S - 1, 0], 1 + rng.permutation(S - 2)])
        else:
            o = rng.permutation(S)
        deg = np.where(t == 0, 0, 3 if full else rng.integers(1, 4, S))
        row = np.stack([o, np.where(deg > 0, o[a], S), np.where(deg > 1, o[b], S), np.where(deg > 2, o[c], S)], axis=1)
        four = np.zeros((S, 4), np.int64); four[at] = rng.permuted(row, axis=1)
        v = np.concatenate([src[g], np.zeros((16, 1), np.int64)], axis=1)
        pk[:, 16 * g:16 * g + 16] = (np.sum(v[:, four], axis=2) & 255).reshape(16, N, P).transpose(1, 0, 2)
        nb[:, g] = four.reshape(N, P, 4).transpose(0, 2, 1)
    return {"packets": pk.astype(BF), "nb": np.stack([gtable(nb[q].reshape(8, 4 * P)) for q in range(N)])}
def anycounts(rng):
    return np.stack([np.stack([counts(rng, R) for g in range(8)]) for q in range(N)])
def setup_inputs(rng):
    return fountain(rng, anycounts(rng), rng.integers(0, 256, (8, 16, S)))
def setup_inputs_caps(rng):
    cnt = anycounts(rng); early = np.zeros(R, np.int64); early[:P // CAP] = CAP; early[P // CAP] = P % CAP
    for g in range(8):
        q = rng.permutation(N); cnt[q[0], g] = early; cnt[q[1], g] = early[::-1]
    cnt[:, rng.integers(0, 8)] = early
    return fountain(rng, cnt, rng.integers(0, 256, (8, 16, S)))
def setup_inputs_short(rng):
    m = rng.permutation(LEAST + np.arange(8) % (R - LEAST + 1)); cnt = np.stack([np.stack([counts(rng, m[g]) for g in range(8)]) for q in range(N)])
    return fountain(rng, cnt, rng.integers(0, 256, (8, 16, S)))
def setup_inputs_hubs(rng):
    return fountain(rng, anycounts(rng), rng.integers(236, 256, (8, 16, S)), e=8, full=True)
def setup_inputs_spread(rng):
    src = np.floor(rng.random((8, 16, S)) * np.exp2(rng.integers(0, 9, (8, 1, S)))) * (rng.random((8, 1, S)) > 0.0625)
    return fountain(rng, anycounts(rng), src.astype(np.int64))
def check_inputs(d):
    bad = []; x = d["packets"].astype(np.float32)
    if not ((x >= 0) & (x <= 255) & (x == np.floor(x))).all():
        bad.append("packets")
    if d["nb"].min() < 0 or d["nb"].max() > S:
        return bad + ["nb"]
    nbr = np.concatenate([gentries(d["nb"][q]).reshape(8, 4, P) for q in range(N)], axis=2).astype(np.int64)
    z = np.sort(nbr, axis=1)
    if ((z[:, 1:] == z[:, :-1]) & (z[:, 1:] < S)).any():
        bad.append("neighbours differ")
    known = np.zeros((8, S + 1), bool); known[:, S] = True; over = False
    for t in range(R):
        for g in range(8):
            un = ~known[g][nbr[g]]; j = np.nonzero(np.sum(un, axis=0) == 1)[0]
            over = over or np.bincount(j // P, minlength=N).max() > CAP
            known[g, np.sum(np.where(un[:, j], nbr[g][:, j], 0), axis=0)] = True
    if over:
        bad.append("cap")
    if not known.all():
        bad.append("all released")
    return bad
def reference(packets, nb):
    nbr = np.concatenate([gentries(nb[q]).reshape(8, 4, P) for q in range(N)], axis=2).astype(np.int64)
    pk = np.concatenate([packets[q].astype(np.float32).reshape(8, 16, P) for q in range(N)], axis=2).astype(np.int64)
    v = np.zeros((8, 16, S + 1), np.int64); known = np.zeros((8, S + 1), bool); known[:, S] = True
    w = np.zeros((8, S + 1), np.int64)
    for t in range(1, R + 1):
        for g in range(8):
            un = ~known[g][nbr[g]]; j = np.nonzero(np.sum(un, axis=0) == 1)[0]; p = nbr[g][:, j]
            s = np.sum(np.where(un[:, j], p, 0), axis=0)
            new = (pk[g][:, j] - np.sum(v[g][:, p], axis=1)) & 255
            v[g][:, s] = new; w[g, s] = t; known[g, s] = True
    y = v[:, :, :S].reshape(128, N, P).transpose(1, 0, 2); u = w[:, :S].reshape(8, N, P).transpose(1, 0, 2)
    return {"y": np.ascontiguousarray(y).astype(np.float32), "rounds": np.ascontiguousarray(u).astype(np.float32)}

@@ -1,0 +1,328 @@
+from concourse.bass import DstId, RemoteDMATransfer
+from concourse.mybir import AluOpType as Op, ActivationFunctionType as Act
+
+N, S, P, R = 8, 8192, 1024, 5
+MARK = -49152.0
+BASE = 10496
+WREL = BASE + S + 1136
+BIG = 1.0e9
+FAR = 1048576.0
+
+SCRATCH = {
+    "stp": ("dram", [N, 128, 128], "bfloat16"), "stn": ("dram", [N, 128, 32], "int32"),
+    "lnp": ("dram", [N, 128, 128], "bfloat16"), "lnn": ("dram", [N, 128, 32], "int32"),
+    "stw": ("dram", [N, 128, 8], "float32"), "lnw": ("dram", [N, 128, 8], "float32"),
+    "pk": ("sbuf", [128, P], "bfloat16"), "nbi": ("sbuf", [128, 4, 64], "int32"),
+    "rel": ("sbuf", [128, WREL], "bfloat16"), "tab": ("sbuf", [128, S + 16], "bfloat16"),
+    "gat": ("sbuf", [128, 4 * P], "bfloat16"),
+    "nba": ("sbuf", [128, 4, 64], "float32"), "nbb": ("sbuf", [128, 4, 64], "float32"),
+    "nbc": ("sbuf", [128, 4, 64], "float32"), "k4": ("sbuf", [128, 4, 64], "float32"),
+    "hi": ("sbuf", [128, 4, 64], "bfloat16"), "lo": ("sbuf", [128, 4, 64], "bfloat16"),
+    "look": ("sbuf", [128, 256], "uint16"), "off": ("sbuf", [128, 64], "uint16"),
+    "m5": ("sbuf", [128, 320], "float32"), "lim": ("sbuf", [128, 320], "float32"),
+    "st5": ("sbuf", [128, 320], "float32"), "slot": ("sbuf", [128, 64], "float32"),
+    "u": ("sbuf", [128, P], "bfloat16"), "val": ("sbuf", [128, P], "bfloat16"),
+    "ja": ("sbuf", [128, 128], "int32"), "jb": ("sbuf", [128, 128], "int32"),
+    "jc": ("sbuf", [128, 128], "int32"), "jd": ("sbuf", [128, 128], "int32"),
+    "eye": ("sbuf", [128, 128], "bfloat16"), "neye": ("sbuf", [128, 128], "bfloat16"),
+    "same": ("sbuf", [128, 128], "bfloat16"), "samef": ("sbuf", [128, 16], "float32"),
+    "wrap": ("sbuf", [128, 16 * 128], "bfloat16"), "lay": ("sbuf", [128, 8 * 128], "bfloat16"),
+    "snap": ("sbuf", [128, 256], "bfloat16"), "sna": ("sbuf", [128, 256], "bfloat16"),
+    "rnd": ("sbuf", [128, 64], "float32"),
+    "msg": ("sbuf", [128, P], "bfloat16"), "land": ("sbuf", [128, P], "bfloat16"),
+    "yf": ("sbuf", [128, P], "float32"),
+    "ps0": ("psum", [128, 16, 64], "float32"), "ps1": ("psum", [128, 16, 64], "float32"),
+    "ps2": ("psum", [128, 16, 64], "float32"), "ps3": ("psum", [128, 16, 64], "float32"),
+}
+SEMAPHORES = (["cv", "ca", "cp", "cg", "stgn", "stgp", "own", "arn", "arp", "arw", "sent", "ldn", "ldp",
+               "snp", "stgw", "ownw", "outa", "outb"] + ["ya%d" % i for i in range(N)])
+
+CHUNKS = [(0, 20), (20, 48), (48, 64)]
+ORDER = {
+    "v": [("g", 0, 0, 4), ("g", 1, 0, 4), ("r", 0, 1), ("r", 0, 0), ("r", 0, 2), ("r", 0, 3), ("u", 0), ("n", 0),
+          ("y", 0), ("o", 0), ("s", 0), ("n", 1), ("y", 1), ("n", 2), ("o", 1), ("o", 2), ("s", 1), ("s", 2)],
+    "a": [("g", 0, 4, 8), ("g", 1, 4, 8), ("g", 2, 0, 8), ("r", 1, 1), ("r", 1, 2), ("r", 1, 3), ("r", 1, 0),
+          ("u", 1), ("r", 2, 3), ("r", 2, 2), ("r", 2, 0), ("r", 2, 1), ("u", 2), ("w", 0), ("y", 2), ("c", 0)],
+    "p": [("X", 0, 3), ("Z", 0), ("X", 0, 1), ("X", 0, 0), ("X", 0, 2), ("Z", 1), ("X", 1, 2), ("X", 1, 3),
+          ("X", 1, 1), ("X", 1, 0), ("Z", 2), ("X", 2, 2), ("X", 2, 0), ("X", 2, 3), ("X", 2, 1), ("D", 2),
+          ("U", 2), ("W", 0)],
+}
+PIECES = [("v", 512), ("a", 576), ("v", 640), ("a", 640), ("v", 640), ("a", 704), ("v", 768), ("a", 768),
+          ("v", 768), ("a", 704), ("v", 896), ("a", 576)]
+FIRST = [("a", 640), ("v", 576), ("a", 832), ("v", 832), ("a", 896), ("v", 896), ("a", 960), ("v", 832),
+         ("a", 1024), ("v", 704)]
+BATCHES = [(0, 2, 4), (2, 4, 4), (4, 6, 4), (6, 7, 8)]
+
+
+def peers(src, cores, topo):
+    def far(r):
+        a, b = topo.chip(cores[src]), topo.chip(cores[r])
+        return 2 if topo.mates(a, b) else (1 if topo.same_plane(a, b) else 0)
+    return sorted([r for r in range(N) if r != src], key=lambda r: (far(r), (r - src) % N))
+
+
+def rank_program(g, core, T, topo):
+    me = T.rank_of(core)
+    if me is None:
+        return
+    cores = list(T.cores)
+    sem = T.sem
+    V, A, PE, SY = g.vector, g.scalar, g.tensor, g.sync
+    queue = {"v": V, "a": A, "p": PE, "s": SY, "g": g}
+    count = {"v": 0, "a": 0, "p": 0, "g": 0}
+    seen = {}
+
+    def done(q, ins):
+        ins.then_inc(sem["c" + q], 1)
+        count[q] += 1
+        return (q, count[q])
+
+    def wait(q, *marks):
+        for src, n in marks:
+            name = "c" + src if src in count else src
+            if seen.get((q, name), 0) < n:
+                queue[q].wait_ge(sem[name], n)
+                seen[(q, name)] = n
+
+    order = peers(me, cores, topo)
+
+    def send(dsts, widths, src_of, dst_ap, sem_name):
+        tr, at = [], 0
+        for r, width in zip(dsts, widths):
+            rid, pid, _ = topo.addr(cores[r])
+            mask = sum(1 << e for e in topo.engines(core, cores[r])[at:at + width])
+            at += width
+            tr.append(RemoteDMATransfer(dst_ids=[DstId(rid=rid, pnc=pid)], dma_engine_mask=mask,
+                                        remote_sem=sem[sem_name], src=src_of(r), dst=dst_ap))
+        g.remote_dma_fused(tr, local_sem=sem.sent)
+        return at
+
+    ps = [T.ps0, T.ps1, T.ps2, T.ps3]
+
+    def psum(buf, col, n):
+        return ps[buf][:, col // 64:(col + n) // 64, :]
+
+    SY.dma_start(T.stn[:], T.nb[:]).then_inc(sem.stgn, 16)
+    A.dma_start(T.stp[:], T.packets[:]).then_inc(sem.stgp, 16)
+    SY.dma_start(T.lnn[me], T.nb[16 * me:16 * me + 16, :]).then_inc(sem.own, 16)
+    SY.dma_start(T.lnp[me], T.packets[16 * me:16 * me + 16, :]).then_inc(sem.own, 16)
+    i_ja = done("g", g.iota(T.ja[:], [[1, 128]], 1024, -1))
+    i_slot = done("g", g.iota(T.slot[:], [[16, 64]], 0, 1, allow_small_or_imprecise_dtypes=True))
+    wait("g", ("stgn", 16))
+    sent = send(order, [1] * 7, lambda r: T.stn[r], T.lnn[me], "arn")
+    wait("g", ("stgp", 16))
+    sent += send(order, [1] * 7, lambda r: T.stp[r], T.lnp[me], "arp")
+    i_k4 = done("g", g.iota(T.k4[:], [[0, 4], [-16, 64]], BASE, -1, allow_small_or_imprecise_dtypes=True))
+    i_jc = done("g", g.iota(T.jc[:], [[1, 128]], 1024, -8))
+    wait("s", ("own", 32), ("arn", N - 1))
+    SY.dma_start(T.nbi[:], T.lnn[:]).then_inc(sem.ldn, 16)
+    wait("s", ("arp", N - 1))
+    SY.dma_start(T.pk[:], T.lnp[:]).then_inc(sem.ldp, 16)
+
+    done("v", V.memset(T.lim[:], BIG))
+    done("v", V.memset(T.m5[:], FAR))
+    m = done("v", V.memset(T.tab[:, S:S + 16], 0.0))
+    wait("v", i_ja, i_slot, m)
+    done("v", V.tensor_scalar(T.neye[:], T.ja[:], 1024.0, -1.0, Op.is_equal, Op.mult))
+    done("v", V.tensor_scalar(T.eye[:], T.ja[:], 1024.0, None, Op.is_equal))
+    done("v", V.tensor_copy(T.lim[:, 0::5], T.slot[:]))
+    done("v", V.tensor_scalar(T.lim[:, 4::5], T.slot[:], float(BASE + S), None, Op.add))
+    m = done("v", V.tensor_scalar(T.jb[:], T.ja[:], 15, None, Op.bitwise_and))
+    wait("v", m)
+    done("v", V.tensor_scalar(T.same[:], T.jb[:], 0.0, None, Op.is_equal))
+    m = done("v", V.tensor_scalar(T.samef[:], T.jb[:, 0:16], 0.0, None, Op.is_equal))
+    wait("a", m)
+    for r in range(16):
+        c_wrap = done("a", A.activation(T.wrap[:, 128 * r:128 * r + 128], T.neye[:], Act.Identity,
+                                        scale=T.samef[:, r:r + 1]))
+    done("v", V.memset(T.rel[:, BASE:BASE + S], MARK))
+    wait("v", i_jc)
+    m = done("v", V.tensor_scalar(T.jd[:], T.jc[:], 127, None, Op.bitwise_and))
+    wait("v", m)
+    for a in range(8):
+        c_lay = done("v", V.tensor_scalar(T.lay[:, 128 * a:128 * a + 128], T.jd[:], float(a), None, Op.is_equal))
+
+    wait("v", ("ldn", 16), i_k4)
+    m_b = done("v", V.tensor_tensor(T.nbb[:], T.nbi[:], T.k4[:], Op.add))
+    m = done("v", V.tensor_scalar(T.nba[:], T.nbi[:], -32768.0, float(S * 32768), Op.mult, Op.add))
+    wait("v", m)
+    for k in range(4):
+        m = done("v", V.tensor_tensor(T.m5[:, 1 + k::5], T.nba[:, k, :], T.nbb[:, k, :], Op.min))
+    wait("v", m)
+    m = done("v", V.tensor_tensor_scan(T.st5[:], T.m5[:], T.lim[:], 0.0, Op.add, Op.min))
+    wait("v", m)
+    m_off = done("v", V.tensor_copy(T.off[:], T.st5[:, 4::5]))
+    wait("a", m_b)
+    m = done("a", A.activation(T.nbc[:], T.nbb[:], Act.Identity, bias=MARK))
+    wait("a", m)
+    m = done("a", A.activation(T.hi[:], T.nbc[:], Act.Identity))
+    wait("v", ("ldp", 16), m_off)
+    last = done("v", V.tensor_copy(T.rel[:, 0:WREL].indirect(T.off[:, 0:64]), T.pk[:]))
+    for c0, c1 in CHUNKS:
+        done("v", V.tensor_copy(T.look[:, 4 * c0:4 * c1], T.nbi[:, :, c0:c1]))
+    wait("v", m)
+    done("v", V.tensor_tensor(T.lo[:], T.nbc[:], T.hi[:], Op.subtract))
+    wait("p", c_wrap, ("ldp", 16))
+
+    def carry(q, dst, src):
+        if q == "v":
+            return done("v", V.tensor_scalar(dst, src, -7 * MARK, None, Op.add))
+        return done("a", A.activation(dst, src, Act.Identity, bias=-7 * MARK))
+
+    def spread(t, scat):
+        wait("p", scat)
+        if t > 1:
+            wait("v", ("snp", 16 * (t - 1)))
+            wait("a", ("snp", 16 * (t - 1)))
+        freed, col, turn, ends = {}, 0, {"v": 0, "a": 0}, {}
+        for q, n in (FIRST if t == 1 else PIECES):
+            buf = 2 * "va".index(q) + turn[q] % 2
+            turn[q] += 1
+            if buf in freed:
+                wait("p", freed[buf])
+            for c in range(0, n, 512):
+                w = min(512, n - c)
+                mm = PE.matmul(psum(buf, c, w), T.same[:], T.rel[:, BASE + col + c:BASE + col + c + w], True, True)
+            wait(q, done("p", mm))
+            freed[buf] = ends[q] = carry(q, T.tab[:, col:col + n], psum(buf, 0, n))
+            col += n
+        ends = list(ends.values())
+        wait("s", *ends)
+        SY.dma_start(T.snap[:, 64 * (t - 1):64 * t], T.tab[0:1, 0:S]).then_inc(sem.snp, 16)
+        return ends
+
+    def peel(t, ends):
+        for q in "vap":
+            wait(q, *ends)
+        plan = {q: [k for k in ORDER[q] if t == R or k[0] not in "wWc"] for q in ORDER}
+        xs = [psum(j // 2, 512 * (j % 2), 16 * (c1 - c0)) for j, (c0, c1) in enumerate(CHUNKS)]
+
+        def zpart(j, k0, k1):
+            return ps[2 + j // 2][:, 8 * (j % 2) + k0:8 * (j % 2) + k1, 0:CHUNKS[j][1] - CHUNKS[j][0]]
+
+        for j, (c0, c1) in enumerate(CHUNKS):
+            PE.matmul(zpart(j, 0, 4), T.eye[:], T.hi[:, :, c0:c1], True, False)
+            PE.matmul(zpart(j, 0, 4), T.eye[:], T.lo[:, :, c0:c1], False, False)
+            PE.matmul(xs[j], T.eye[:], T.pk[:, 16 * c0:16 * c1], True, False)
+        mark, scats = {}, []
+        lists = [k for q in "va" for k in ORDER[q] if k[0] == "g"]
+
+        def needs(q, k):
+            j = k[1]
+            if k[0] in "gw":
+                return []
+            if k[0] == "X":
+                return [d for d in lists if d[1] == j and d[2] < 2 * k[2] + 2 and d[3] > 2 * k[2]]
+            if k[0] in "ZD":
+                return [d for d in lists if d[1] == j]
+            return {"u": [("X", j, d) for d in range(4)], "U": [("u", j)], "n": [("r", j, d) for d in range(4)],
+                    "r": [("Z", j)], "o": [("n", j)], "y": [("U" if q == "a" else "u", j)],
+                    "s": [("y", j), ("o", j)], "W": [("w", j)], "c": [("W", j)]}[k[0]]
+
+        def emit(q, k):
+            j = k[1]
+            c0, c1 = CHUNKS[j]
+            n = c1 - c0
+            x, u, val = xs[j], T.u[:, 16 * c0:16 * c1], T.val[:, 16 * c0:16 * c1]
+            twin = psum(1, 512, 16 * n)
+
+            def place(i):
+                return T.gat[:, 64 * c0 + 16 * n * i:64 * c0 + 16 * n * (i + 1)]
+
+            if k[0] == "w":
+                wait(q, ("snp", 64))
+                return done(q, A.activation(T.sna[:], T.snap[:], Act.Relu, scale=1.0 / MARK))
+            if k[0] == "W":
+                for i in range(4):
+                    mm = PE.matmul(psum(3, 512, 64), T.eye[:], T.sna[:, 64 * i:64 * i + 64], i == 0, i == 3)
+                return done(q, mm)
+            if k[0] == "c":
+                return done(q, A.activation(T.rnd[:], psum(3, 512, 64), Act.Identity, bias=1.0))
+            if k[0] == "g":
+                a, b = 4 * c0 + k[2] * n // 2, 4 * c0 + k[3] * n // 2
+                src, dst = T.tab[:, 0:S + 1].indirect(T.look[:, a:b]), T.gat[:, 16 * a:16 * b]
+                return done(q, V.tensor_copy(dst, src) if q == "v" else A.activation(dst, src, Act.Identity))
+            if k[0] == "X":
+                end = k == [d for d in ORDER["p"] if d[:2] == k[:2]][-1]
+                return done(q, PE.matmul(x, T.neye[:], place(k[2]), False, end))
+            if k[0] == "Z":
+                for r in range(16):
+                    mm = PE.matmul(zpart(j, 0, 4), T.wrap[:, 128 * r:128 * r + 128],
+                                   T.gat[:, 64 * c0 + r:64 * c1:16], False, r == 15)
+                return done(q, mm)
+            if k[0] == "D":
+                PE.matmul(twin, T.eye[:], T.pk[:, 16 * c0:16 * c1], True, False)
+                for i in range(4):
+                    mm = PE.matmul(twin, T.neye[:], place(i), False, False)
+                return done(q, mm)
+            if k[0] == "U":
+                return done(q, PE.matmul(twin, T.neye[:], u, False, True))
+            if k[0] == "r":
+                m5, z = T.m5[:, 5 * c0 + 1 + k[2]:5 * c1:5], zpart(j, k[2], k[2] + 1)
+                return done(q, A.activation(m5, z, Act.Relu) if q == "a" else
+                            V.tensor_scalar(m5, z, 0.0, None, Op.max))
+            if k[0] == "n":
+                return done(q, V.tensor_tensor_scan(T.st5[:, 5 * c0:5 * c1], T.m5[:, 5 * c0:5 * c1],
+                                                    T.lim[:, 5 * c0:5 * c1], 0.0, Op.add, Op.min))
+            if k[0] == "o":
+                return done(q, V.tensor_copy(T.off[:, c0:c1], T.st5[:, 5 * c0 + 4:5 * c1:5]))
+            if k[0] == "u":
+                return done(q, A.activation(u, x, Act.Identity, bias=-127.5) if q == "a" else
+                            V.tensor_scalar(u, x, -127.5, None, Op.add))
+            if k[0] == "y":
+                return done(q, A.activation(val, twin, Act.Identity) if q == "a" else
+                            V.tensor_tensor(val, x, u, Op.subtract))
+            wait(q, *scats)
+            scats.append(done(q, V.tensor_copy(T.rel[:, 0:WREL].indirect(T.off[:, c0:c1]), val)))
+            return scats[-1]
+
+        at = {"v": 0, "a": 0, "p": 0}
+        while any(at[q] < len(plan[q]) for q in at):
+            for q in at:
+                while at[q] < len(plan[q]) and all(d in mark for d in needs(q, plan[q][at[q]])):
+                    k = plan[q][at[q]]
+                    wait(q, *[mark[d] for d in needs(q, k)])
+                    mark[k] = emit(q, k)
+                    at[q] += 1
+        return scats[-1], mark
+
+    for t in range(1, R):
+        last, mark = peel(t + 1, spread(t, last))
+
+    wait("s", mark[("c", 0)])
+    SY.dma_start(T.stw[:], T.rnd[:]).then_inc(sem.stgw, 16)
+    SY.dma_start(T.lnw[me], T.rnd[16 * me:16 * me + 16, :]).then_inc(sem.ownw, 16)
+    wait("g", ("stgw", 16))
+    sent += send(order, [2] + [1] * 6, lambda r: T.stw[r], T.lnw[me], "arw")
+    wait("p", last, c_lay, mark[("c", 0)])
+    made = {}
+    for b, r in enumerate(order + [me]):
+        out = psum(b // 2, 512 * (b % 2), 128)
+        for a in range(8):
+            col = BASE + P * r + 128 * a
+            mm = PE.matmul(out, T.lay[:, 128 * a:128 * a + 128], T.rel[:, col:col + 128], a == 0, a == 7)
+        q = "va"[b % 2]
+        wait(q, done("p", mm))
+        made[r] = carry(q, (T.yf if r == me else T.msg)[:, 128 * r:128 * r + 128], out)
+    for first, end, width in BATCHES:
+        wait("g", *[made[r] for r in order[first:end]])
+        sent += send(order[first:end], [width] * (end - first), lambda r: T.msg[:, 128 * r:128 * r + 128],
+                     T.land[:, 128 * me:128 * me + 128], "ya%d" % me)
+    stores = {"s": 0, "a": 0}
+
+    def store(q, r, made_by):
+        wait(q, made_by)
+        queue[q].dma_start(T.y[16 * r:16 * r + 16, :], T.yf[:, 128 * r:128 * r + 128]).then_inc(
+            sem.outa if q == "s" else sem.outb, 16)
+        stores[q] += 16
+
+    store("s", me, made[me])
+    turn = {r: peers(r, cores, topo).index(me) for r in order}
+    for i, r in enumerate(sorted(order, key=lambda r: turn[r])):
+        wait("v", ("ya%d" % r, [w for first, end, w in BATCHES if first <= turn[r] < end][0]))
+        store("as"[i % 2], r, done("v", V.tensor_copy(T.yf[:, 128 * r:128 * r + 128], T.land[:, 128 * r:128 * r + 128])))
+    wait("s", ("ownw", 16), ("arw", N - 1 + sum(1 for r in order if turn[r] == 0)))
+    SY.dma_start(T.rounds[:], T.lnw[:]).then_inc(sem.outa, 16)
+    wait("s", ("outa", stores["s"] + 16))
+    wait("a", ("outb", stores["a"]))
+    wait("g", ("sent", sent), ("v", count["v"]), ("a", count["a"]), ("p", count["p"]), ("g", count["g"]))

@@ -3,55 +3,85 @@ from concourse.mybir import AluOpType as Op, ActivationFunctionType as Act
 
 N, S, P, R = 8, 8192, 1024, 5
 MARK = -49152.0
-BASE = 10496
+BASE = 16384
 WREL = BASE + S + 1136
+KEPT = 2048
+LEFT = 36
+FILL = 2048
 BIG = 1.0e9
 FAR = 1048576.0
+DEG = 32768.0
+CUT = 57344.0
+AWAY = 32768.0
 
 SCRATCH = {
-    "stp": ("dram", [N, 128, 128], "bfloat16"), "stn": ("dram", [N, 128, 32], "int32"),
-    "lnp": ("dram", [N, 128, 128], "bfloat16"), "lnn": ("dram", [N, 128, 32], "int32"),
-    "stw": ("dram", [N, 128, 8], "float32"), "lnw": ("dram", [N, 128, 8], "float32"),
     "pk": ("sbuf", [128, P], "bfloat16"), "nbi": ("sbuf", [128, 4, 64], "int32"),
     "rel": ("sbuf", [128, WREL], "bfloat16"), "tab": ("sbuf", [128, S + 16], "bfloat16"),
-    "gat": ("sbuf", [128, 4 * P], "bfloat16"),
-    "nba": ("sbuf", [128, 4, 64], "float32"), "nbb": ("sbuf", [128, 4, 64], "float32"),
-    "nbc": ("sbuf", [128, 4, 64], "float32"), "k4": ("sbuf", [128, 4, 64], "float32"),
-    "hi": ("sbuf", [128, 4, 64], "bfloat16"), "lo": ("sbuf", [128, 4, 64], "bfloat16"),
-    "look": ("sbuf", [128, 256], "uint16"), "off": ("sbuf", [128, 64], "uint16"),
+    "gat": ("sbuf", [128, P, 4], "bfloat16"),
+    "sum2": ("sbuf", [128, 128], "float32"), "sum1": ("sbuf", [128, 64], "float32"),
+    "one": ("sbuf", [128, 64], "float32"), "top": ("sbuf", [128, 64], "float32"),
+    "off": ("sbuf", [128, 64], "uint16"), "look": ("sbuf", [128, 256], "uint16"),
+    "hl": ("sbuf", [128, 128, 4], "bfloat16"),
     "m5": ("sbuf", [128, 320], "float32"), "lim": ("sbuf", [128, 320], "float32"),
     "st5": ("sbuf", [128, 320], "float32"), "slot": ("sbuf", [128, 64], "float32"),
     "u": ("sbuf", [128, P], "bfloat16"), "val": ("sbuf", [128, P], "bfloat16"),
-    "ja": ("sbuf", [128, 128], "int32"), "jb": ("sbuf", [128, 128], "int32"),
-    "jc": ("sbuf", [128, 128], "int32"), "jd": ("sbuf", [128, 128], "int32"),
-    "eye": ("sbuf", [128, 128], "bfloat16"), "neye": ("sbuf", [128, 128], "bfloat16"),
+    "jw": ("sbuf", [128, 160], "int32"), "jb": ("sbuf", [128, 128], "int32"),
+    "eyew": ("sbuf", [128, 160], "bfloat16"), "eye": ("sbuf", [128, 128], "bfloat16"),
+    "neye": ("sbuf", [128, 128], "bfloat16"),
     "same": ("sbuf", [128, 128], "bfloat16"), "samef": ("sbuf", [128, 16], "float32"),
-    "wrap": ("sbuf", [128, 16 * 128], "bfloat16"), "lay": ("sbuf", [128, 8 * 128], "bfloat16"),
-    "snap": ("sbuf", [128, 256], "bfloat16"), "sna": ("sbuf", [128, 256], "bfloat16"),
-    "rnd": ("sbuf", [128, 64], "float32"),
-    "msg": ("sbuf", [128, P], "bfloat16"), "land": ("sbuf", [128, P], "bfloat16"),
+    "wrap": ("sbuf", [128, 16 * 128], "bfloat16"),
+    "sl": ("sbuf", [128, 128], "bfloat16"), "sr": ("sbuf", [128, 320], "bfloat16"),
+    "pi": ("sbuf", [128, 2], "int32"), "pf": ("sbuf", [128, 6], "float32"), "blk": ("sbuf", [128, 128], "bfloat16"),
+    "rank": ("sbuf", [128, 3, 128], "bfloat16"), "hop": ("sbuf", [128, 4, 160], "bfloat16"),
+    "dig": ("sbuf", [128, 64, 16], "float32"), "nbf": ("sbuf", [128, 4, 64], "float32"),
+    "eyef": ("sbuf", [128, 128], "float32"),
+    "cut": ("sbuf", [128, P], "float32"),
+    "flag": ("sbuf", [128, 66], "bfloat16"), "eight": ("sbuf", [128, 64], "float32"),
+    "cand": ("sbuf", [128, 64], "float32"), "kept": ("sbuf", [128, LEFT // 2, 32], "bfloat16"),
+    "look2": ("sbuf", [128, 5 * LEFT], "uint16"), "pk2": ("sbuf", [128, 16 * LEFT], "bfloat16"),
+    "snap": ("sbuf", [128, 4, 64], "bfloat16"), "rnd": ("sbuf", [128, 64], "float32"),
+    "msg": ("sbuf", [128, N, 128], "bfloat16"), "land": ("sbuf", [128, N, 128], "bfloat16"),
     "yf": ("sbuf", [128, P], "float32"),
-    "ps0": ("psum", [128, 16, 64], "float32"), "ps1": ("psum", [128, 16, 64], "float32"),
-    "ps2": ("psum", [128, 16, 64], "float32"), "ps3": ("psum", [128, 16, 64], "float32"),
+    "ps0": ("psum", [128, 128, 8], "float32"), "ps1": ("psum", [128, 128, 8], "float32"),
+    "ps2": ("psum", [128, 128, 8], "float32"), "ps3": ("psum", [128, 128, 8], "float32"),
 }
-SEMAPHORES = (["cv", "ca", "cp", "cg", "stgn", "stgp", "own", "arn", "arp", "arw", "sent", "ldn", "ldp",
-               "snp", "stgw", "ownw", "outa", "outb"] + ["ya%d" % i for i in range(N)])
+PARTS = {"n": ("int32", 32), "p": ("bfloat16", 128), "w": ("float32", 8)}
+for _k, (_d, _w) in PARTS.items():
+    SCRATCH["st_" + _k] = ("dram", [N, 128, _w], _d)
+    SCRATCH["ln_" + _k] = ("dram", [N, 128, _w], _d)
+SEMAPHORES = (["cv", "ca", "cp", "cg", "sent", "snp", "outa", "outb"] + ["ya%d" % i for i in range(N)]
+              + [a + k for k in PARTS for a in ("stg", "arr", "ld")])
 
-CHUNKS = [(0, 20), (20, 48), (48, 64)]
 ORDER = {
-    "v": [("g", 0, 0, 4), ("g", 1, 0, 4), ("r", 0, 1), ("r", 0, 0), ("r", 0, 2), ("r", 0, 3), ("u", 0), ("n", 0),
-          ("y", 0), ("o", 0), ("s", 0), ("n", 1), ("y", 1), ("n", 2), ("o", 1), ("o", 2), ("s", 1), ("s", 2)],
-    "a": [("g", 0, 4, 8), ("g", 1, 4, 8), ("g", 2, 0, 8), ("r", 1, 1), ("r", 1, 2), ("r", 1, 3), ("r", 1, 0),
-          ("u", 1), ("r", 2, 3), ("r", 2, 2), ("r", 2, 0), ("r", 2, 1), ("u", 2), ("w", 0), ("y", 2), ("c", 0)],
-    "p": [("X", 0, 3), ("Z", 0), ("X", 0, 1), ("X", 0, 0), ("X", 0, 2), ("Z", 1), ("X", 1, 2), ("X", 1, 3),
-          ("X", 1, 1), ("X", 1, 0), ("Z", 2), ("X", 2, 2), ("X", 2, 0), ("X", 2, 3), ("X", 2, 1), ("D", 2),
-          ("U", 2), ("W", 0)],
+    2: {"v": "g0-20.2 g0-20.1 g20-48.2 g20-48.1 r0-20 u0-20 g48-64.0 n0-20 y0-20 o0-20 s0-20 n20-48 y20-48 "
+             "o20-48 n48-64 s20-48 o48-64 s48-64",
+        "a": "g0-20.0 g0-20.3 g20-48.0 g20-48.3 g48-64.3 g48-64.1 g48-64.2 r20-48 u20-48 r48-64 u48-64 y48-64 "
+             "C0-64",
+        "p": "K0-20 B0-20 B20-48 K20-48 B48-64 K48-64 X0-20.2 X0-20.0 Z0-20 X0-20.3 X0-20.1 X20-48.0 X20-48.2 "
+             "Z20-48 X20-48.3 X20-48.1 X48-64.3 Z48-64 X48-64.1 X48-64.0 X48-64.2 D48-64 U48-64 E0-64"},
+    3: {"v": "g0-18.1 g0-18.0 g18-44.2 g18-44.1 r0-18 n0-18 m0-18 u0-18 y0-18 q0-18 j0-18 m18-44 o0-18 s0-18 "
+             "n18-44 r44-64 n44-64 y18-44 m44-64 q18-44 j18-44 q44-64 o18-44 j44-64 s18-44 o44-64 y44-64 s44-64",
+        "a": "g0-18.3 g0-18.2 g18-44.3 g18-44.0 g44-64.1 f0-18 g44-64.3 g44-64.0 g44-64.2 r18-44 u18-44 f18-44 "
+             "f44-64 u44-64",
+        "p": "K0-18 B0-18 K18-44 B18-44 B44-64 K44-64 X0-18.1 X0-18.3 Z0-18 X0-18.0 X0-18.2 X18-44.2 X18-44.3 "
+             "X18-44.1 P0-18 X18-44.0 Z18-44 Z44-64 X44-64.2 X44-64.3 X44-64.1 X44-64.0 P18-44 P44-64"},
+    4: {"v": "g0-16.0 g0-16.1 g16-36.1 g16-36.0 r0-16 n0-16 o0-16 y0-16 s0-16 y16-36 n16-36 o16-36 s16-36",
+        "a": "g0-16.2 g0-16.3 g16-36.2 g16-36.3 u0-16 u16-36 r16-36",
+        "p": "K0-16 B0-16 K16-36 B16-36 X0-16.2 X0-16.0 X0-16.1 X0-16.3 Z0-16 X16-36.2 X16-36.1 X16-36.3 "
+             "X16-36.0 Z16-36"},
 }
-PIECES = [("v", 512), ("a", 576), ("v", 640), ("a", 640), ("v", 640), ("a", 704), ("v", 768), ("a", 768),
-          ("v", 768), ("a", 704), ("v", 896), ("a", 576)]
-FIRST = [("a", 640), ("v", 576), ("a", 832), ("v", 832), ("a", 896), ("v", 896), ("a", 960), ("v", 832),
-         ("a", 1024), ("v", 704)]
-BATCHES = [(0, 2, 4), (2, 4, 4), (4, 6, 4), (6, 7, 8)]
+ORDER[5] = {"v": ORDER[4]["v"], "a": ORDER[4]["a"] + " c0-16", "p": ORDER[4]["p"] + " W0-16"}
+PIECES = {
+    1: "a512 v704 a672 v768 a896 v960 a992 v960 a1024 v704",
+    2: "a576 R v480 a832 v928 a864 v960 a960 v896 a1024 v672",
+    3: "T a512 v256 E a320 L v480 G v928 a960 v864 a512 v960 a960 v928 a512",
+    4: "v448 a512 v640 a672 v704 a576 v832 a736 v928 a768 v800 a576",
+}
+BATCHES = [(0, 2, 4), (2, 6, 2), (6, 7, 8)]
+
+
+def tasks(text):
+    return [(w[0],) + tuple(int(n) for n in (w[1:] + ".0").replace("-", ".").split(".")[:3]) for w in text.split()]
 
 
 def peers(src, cores, topo):
@@ -84,194 +114,307 @@ def rank_program(g, core, T, topo):
                 queue[q].wait_ge(sem[name], n)
                 seen[(q, name)] = n
 
+    def step(ins, *marks):
+        wait("v", ("v", count["v"]), *marks)
+        return done("v", ins())
+
+    def iota(out, pattern, base, by):
+        if count["g"] >= 3:
+            wait("g", ("g", count["g"]))
+        return done("g", g.iota(out, pattern, base, by, allow_small_or_imprecise_dtypes=True))
+
     order = peers(me, cores, topo)
 
-    def send(dsts, widths, src_of, dst_ap, sem_name):
-        tr, at = [], 0
-        for r, width in zip(dsts, widths):
+    def send(dsts, width, src_of, dst_ap, sem_name):
+        tr = []
+        for i, r in enumerate(dsts):
             rid, pid, _ = topo.addr(cores[r])
-            mask = sum(1 << e for e in topo.engines(core, cores[r])[at:at + width])
-            at += width
+            mask = sum(1 << e for e in topo.engines(core, cores[r])[i * width:(i + 1) * width])
             tr.append(RemoteDMATransfer(dst_ids=[DstId(rid=rid, pnc=pid)], dma_engine_mask=mask,
                                         remote_sem=sem[sem_name], src=src_of(r), dst=dst_ap))
         g.remote_dma_fused(tr, local_sem=sem.sent)
-        return at
+        return width * len(dsts)
 
     ps = [T.ps0, T.ps1, T.ps2, T.ps3]
 
-    def psum(buf, col, n):
-        return ps[buf][:, col // 64:(col + n) // 64, :]
+    def rows(b, first, end, cols, by=1):
+        return ps[b // 2][:, 64 * (b % 2) + first:64 * (b % 2) + end:by, cols]
 
-    SY.dma_start(T.stn[:], T.nb[:]).then_inc(sem.stgn, 16)
-    A.dma_start(T.stp[:], T.packets[:]).then_inc(sem.stgp, 16)
-    SY.dma_start(T.lnn[me], T.nb[16 * me:16 * me + 16, :]).then_inc(sem.own, 16)
-    SY.dma_start(T.lnp[me], T.packets[16 * me:16 * me + 16, :]).then_inc(sem.own, 16)
-    i_ja = done("g", g.iota(T.ja[:], [[1, 128]], 1024, -1))
-    i_slot = done("g", g.iota(T.slot[:], [[16, 64]], 0, 1, allow_small_or_imprecise_dtypes=True))
-    wait("g", ("stgn", 16))
-    sent = send(order, [1] * 7, lambda r: T.stn[r], T.lnn[me], "arn")
-    wait("g", ("stgp", 16))
-    sent += send(order, [1] * 7, lambda r: T.stp[r], T.lnp[me], "arp")
-    i_k4 = done("g", g.iota(T.k4[:], [[0, 4], [-16, 64]], BASE, -1, allow_small_or_imprecise_dtypes=True))
-    i_jc = done("g", g.iota(T.jc[:], [[1, 128]], 1024, -8))
-    wait("s", ("own", 32), ("arn", N - 1))
-    SY.dma_start(T.nbi[:], T.lnn[:]).then_inc(sem.ldn, 16)
-    wait("s", ("arp", N - 1))
-    SY.dma_start(T.pk[:], T.lnp[:]).then_inc(sem.ldp, 16)
+    def bank(b, col, n):
+        return rows(b, col // 8, (col + n) // 8, slice(0, 8))
 
-    done("v", V.memset(T.lim[:], BIG))
-    done("v", V.memset(T.m5[:], FAR))
-    m = done("v", V.memset(T.tab[:, S:S + 16], 0.0))
-    wait("v", i_ja, i_slot, m)
-    done("v", V.tensor_scalar(T.neye[:], T.ja[:], 1024.0, -1.0, Op.is_equal, Op.mult))
-    done("v", V.tensor_scalar(T.eye[:], T.ja[:], 1024.0, None, Op.is_equal))
-    done("v", V.tensor_copy(T.lim[:, 0::5], T.slot[:]))
-    done("v", V.tensor_scalar(T.lim[:, 4::5], T.slot[:], float(BASE + S), None, Op.add))
-    m = done("v", V.tensor_scalar(T.jb[:], T.ja[:], 15, None, Op.bitwise_and))
-    wait("v", m)
-    done("v", V.tensor_scalar(T.same[:], T.jb[:], 0.0, None, Op.is_equal))
-    m = done("v", V.tensor_scalar(T.samef[:], T.jb[:, 0:16], 0.0, None, Op.is_equal))
+    def stage(*parts):
+        for k, src in parts:
+            SY.dma_start(T["st_" + k][:], src[:]).then_inc(sem["stg" + k], 16)
+        for k, src in parts:
+            SY.dma_start(T["ln_" + k][me], src[16 * me:16 * me + 16, :]).then_inc(sem["arr" + k], 16)
+
+    def deal(k):
+        wait("g", ("stg" + k, 16))
+        return send(order, 1, lambda r: T["st_" + k][r], T["ln_" + k][me], "arr" + k)
+
+    def load(q, k, dst):
+        wait(q, ("arr" + k, 16 + N - 1))
+        queue[q].dma_start(dst, T["ln_" + k][:]).then_inc(sem["ld" + k], 16)
+
+    stage(("n", T.nb), ("p", T.packets))
+    iota(T.jw[:], [[1, 160]], 1008, -1)
+    iota(T.slot[:], [[16, 64]], 0, 1)
+    i_a = iota(T.pi[:, 0:1], [[0, 1]], 0, 1)
+    sent = deal("n") + deal("p")
+    load("s", "n", T.nbi[:])
+    load("s", "p", T.pk[:])
+
+    ja = T.jw[:, 16:144]
+    wait("a", done("v", V.memset(T.rel[:, BASE:BASE + FILL], MARK)))
+    m_fill = done("a", A.activation(T.rel[:, BASE + FILL:BASE + 2 * FILL], T.rel[:, BASE:BASE + FILL], Act.Identity))
+    for ap, value in ((T.lim[:], BIG), (T.sl[0:1, :], 1.0), (T.dig[:, :, 10:16], CUT), (T.eight[:], 8.0),
+                      (T.flag[:], -1.0), (T.tab[:, S:S + 16], 0.0), (T.rel[:, KEPT:KEPT + 16 * LEFT], 64.0),
+                      (T.blk[:], 0.5), (T.rank[:, 2, :], AWAY / 2)):
+        m = done("v", V.memset(ap, value))
+    wait("g", m)
+    iota(T.sr[0:1, :], [[-16, 64], [0, 5]], 0, 0)
+    iota(T.sr[0:1, 0::5], [[0, 64]], int(FAR), 0)
+    iota(T.pf[:, 4:5], [[0, 1]], 0, -1)
+    i_slot = iota(T.pf[:, 5:6], [[0, 1]], BASE + int(MARK) - 64, -1)
+    iota(T.dig[:, :, 8], [[1, 8], [0, 8]], int(CUT) + 64, 0)
+    for first in range(0, 128, 32):
+        i_dig = iota(T.dig[first:first + 32, :, 9], [[0, 8], [32, 4], [0, 2]], int(CUT) + 64, 1)
+    for out, of, pattern, test, fill, base, by in (
+            (T.blk[:], T.blk[:], [[-16, 8], [0, 16]], Op.is_ge, 0.0, 0, 1),
+            (T.blk[:], T.blk[:], [[16, 8], [0, 16]], Op.is_ge, 0.0, 15, -1),
+            (T.rank[:, 0, :], T.blk[:], [[1, 128]], Op.is_gt, 0.0, 0, -1),
+            (T.rank[:, 0, :], T.rank[:, 0, :], [[1, 128]], Op.not_equal, -AWAY / 2, 0, -1),
+            (T.rank[:, 1, :], T.blk[:], [[-1, 128]], Op.is_ge, 0.0, 0, 1),
+            (T.rank[:, 2, :], T.rank[:, 2, :], [[1, 128]], Op.is_equal, 0.0, 0, -1)):
+        wait("g", ("g", count["g"]))
+        i_all = done("g", g.affine_select(out, of, pattern, test, fill, base, by))
+    step(lambda: V.tensor_scalar(T.eyew[:], T.jw[:], 1024.0, None, Op.is_equal), i_a)
+    done("v", V.tensor_scalar(T.jb[:], ja, 15, None, Op.bitwise_and))
+    done("v", V.tensor_scalar(T.pi[:, 1:2], T.pi[:, 0:1], 4, 1, Op.arith_shift_right, Op.bitwise_and))
+    step(lambda: V.tensor_scalar(T.samef[:], T.jb[:, 0:16], 0.0, -1.0, Op.is_equal, Op.mult))
+    for i in range(4):
+        m = done("v", V.tensor_scalar(T.pf[:, i:i + 1], T.pi[:, 1:2], float(i % 2), 128.0 ** (i // 2),
+                                      Op.is_equal, Op.mult))
     wait("a", m)
+    made = [(T.hop[:, i, :], T.eyew[:], T.pf[:, i:i + 1], 0.0) for i in range(4)]
+    made += [(T.eye[:], T.eyew[:, 16:144], 1.0, 0.0), (T.eyef[:], T.eyew[:, 16:144], 1.0, 0.0),
+             (T.neye[:], T.eyew[:, 16:144], -1.0, 0.0),
+             (T.lim[:, 0::5], T.slot[:], 1.0, 0.0), (T.lim[:, 4::5], T.slot[:], 1.0, float(BASE + S))]
+    for out, of, scale, bias in made:
+        c_hop = done("a", A.activation(out, of, Act.Identity, bias=bias, scale=scale))
     for r in range(16):
-        c_wrap = done("a", A.activation(T.wrap[:, 128 * r:128 * r + 128], T.neye[:], Act.Identity,
+        c_wrap = done("a", A.activation(T.wrap[:, 128 * r:128 * r + 128], T.eyew[:, 16:144], Act.Identity,
                                         scale=T.samef[:, r:r + 1]))
-    done("v", V.memset(T.rel[:, BASE:BASE + S], MARK))
-    wait("v", i_jc)
-    m = done("v", V.tensor_scalar(T.jd[:], T.jc[:], 127, None, Op.bitwise_and))
-    wait("v", m)
-    for a in range(8):
-        c_lay = done("v", V.tensor_scalar(T.lay[:, 128 * a:128 * a + 128], T.jd[:], float(a), None, Op.is_equal))
+    done("v", V.tensor_scalar(T.same[:], T.jb[:], 0.0, None, Op.is_equal))
+    done("v", V.tensor_scalar(T.top[:], T.slot[:], 4.0 * S + DEG, None, Op.add))
+    done("v", V.memset(T.rel[:, BASE + 2 * FILL:BASE + S], MARK))
 
-    wait("v", ("ldn", 16), i_k4)
-    m_b = done("v", V.tensor_tensor(T.nbb[:], T.nbi[:], T.k4[:], Op.add))
-    m = done("v", V.tensor_scalar(T.nba[:], T.nbi[:], -32768.0, float(S * 32768), Op.mult, Op.add))
-    wait("v", m)
-    for k in range(4):
-        m = done("v", V.tensor_tensor(T.m5[:, 1 + k::5], T.nba[:, k, :], T.nbb[:, k, :], Op.min))
-    wait("v", m)
-    m = done("v", V.tensor_tensor_scan(T.st5[:], T.m5[:], T.lim[:], 0.0, Op.add, Op.min))
-    wait("v", m)
-    m_off = done("v", V.tensor_copy(T.off[:], T.st5[:, 4::5]))
-    wait("a", m_b)
-    m = done("a", A.activation(T.nbc[:], T.nbb[:], Act.Identity, bias=MARK))
-    wait("a", m)
-    m = done("a", A.activation(T.hi[:], T.nbc[:], Act.Identity))
-    wait("v", ("ldp", 16), m_off)
-    last = done("v", V.tensor_copy(T.rel[:, 0:WREL].indirect(T.off[:, 0:64]), T.pk[:]))
-    for c0, c1 in CHUNKS:
-        done("v", V.tensor_copy(T.look[:, 4 * c0:4 * c1], T.nbi[:, :, c0:c1]))
-    wait("v", m)
-    done("v", V.tensor_tensor(T.lo[:], T.nbc[:], T.hi[:], Op.subtract))
-    wait("p", c_wrap, ("ldp", 16))
+    def hop(b, to, big):
+        return T.hop[:, 2 * big + b, 16 - 16 * (to - b):144 - 16 * (to - b)]
+
+    step(lambda: V.tensor_scalar(bank(0, 0, 256), T.nbi[:], float(S), DEG, Op.is_lt, Op.mult), ("ldn", 16))
+    step(lambda: V.tensor_tensor(T.sum2[:], bank(0, 0, 128), T.nbi[:, 0:2, :], Op.add))
+    done("v", V.tensor_tensor(bank(1, 0, 128), bank(0, 128, 128), T.nbi[:, 2:4, :], Op.add))
+    step(lambda: V.tensor_tensor(T.sum1[:], bank(1, 0, 64), T.sum2[:, 0:64], Op.add))
+    done("v", V.tensor_tensor(bank(0, 0, 64), bank(1, 64, 64), T.sum2[:, 64:128], Op.add))
+    step(lambda: V.tensor_tensor(bank(1, 0, 64), bank(0, 0, 64), T.sum1[:], Op.add))
+    step(lambda: V.tensor_tensor(T.one[:], bank(1, 0, 64), T.top[:], Op.min))
+    m_off = step(lambda: V.tensor_scalar(T.off[:], T.one[:], BASE - 3.0 * S - DEG, None, Op.add))
+    m = done("v", V.tensor_copy(T.nbf[:], T.nbi[:]))
+    wait("v", m_off, m_fill, ("ldp", 16))
+    last = done("v", V.tensor_copy(T.rel[:, 0:WREL].indirect(T.off[:]), T.pk[:]))
+    done("v", V.tensor_copy(T.look[:], T.nbi[:]))
+    wait("p", m, c_hop)
+    for part in range(2):
+        if part:
+            wait("p", m_parts)
+            PE.matmul(rows(7, 0, 64, slice(0, 4)), T.neye[:], T.hl[:, 0:64, :], True, False)
+        for k in range(4):
+            mm = PE.matmul(rows(6 + part, 0, 64, k), T.eyef[:], T.nbf[:, k, :], not part, not part or k == 3)
+        wait("a", done("p", mm))
+        m_parts = done("a", A.activation(T.hl[:, 64 * part:64 * part + 64, :], rows(6 + part, 0, 64, slice(0, 4)),
+                                         Act.Identity, bias=BASE + MARK))
 
     def carry(q, dst, src):
         if q == "v":
             return done("v", V.tensor_scalar(dst, src, -7 * MARK, None, Op.add))
         return done("a", A.activation(dst, src, Act.Identity, bias=-7 * MARK))
 
+    ready, busy = [], {3: m_parts}
+
+    def lists(kind, before):
+        if kind == "R":
+            wait("v", i_dig, *busy.values())
+            return done("v", V.transpose(T.cut[:], T.dig[:]))
+        if kind == "T":
+            wait("v", before)
+            return done("v", V.transpose(T.kept[:], T.rel[:, KEPT:KEPT + 16 * LEFT]))
+        if kind == "E":
+            wait("p", before)
+            return done("p", digits(lambda b: rows(7, b, LEFT, slice(0, 5), 2), 0, LEFT, 5, True))
+        if kind == "L":
+            wait("v", before)
+            for k in (4, 0, 1, 2, 3):
+                m = done("v", V.tensor_scalar(T.look2[:, LEFT * k:LEFT * k + LEFT], rows(7, 0, LEFT, k),
+                                              -64.0 * (129 if k == 4 else 1), None, Op.add))
+                if k == 4:
+                    numbers = m
+            ready.append(m)
+            return numbers
+        wait("a", before)
+        return done("a", A.activation(T.pk2[:], T.pk[:, 0:P].indirect(T.look2[:, 4 * LEFT:5 * LEFT]), Act.Identity))
+
+    def digits(out, c0, c1, n, alone):
+        for b in range(2):
+            for i in range(4):
+                par, low = i // 2, i % 2
+                mm = PE.matmul(out(b), hop(b, par, 1 - low),
+                               T.kept[:, c0 // 2:c1 // 2, 16 * par + low:16 * par + 2 * n:2],
+                               alone and i == 0, alone and i == 3)
+        return mm
+
     def spread(t, scat):
         wait("p", scat)
         if t > 1:
             wait("v", ("snp", 16 * (t - 1)))
             wait("a", ("snp", 16 * (t - 1)))
-        freed, col, turn, ends = {}, 0, {"v": 0, "a": 0}, {}
-        for q, n in (FIRST if t == 1 else PIECES):
+        freed, col, turn, side = dict(busy), 0, {"v": 0, "a": 0}, scat
+        for piece in PIECES[t].split():
+            if len(piece) == 1:
+                side = lists(piece, side)
+                continue
+            q, n = piece[0], int(piece[1:])
             buf = 2 * "va".index(q) + turn[q] % 2
             turn[q] += 1
             if buf in freed:
-                wait("p", freed[buf])
+                wait("p", freed.pop(buf))
             for c in range(0, n, 512):
                 w = min(512, n - c)
-                mm = PE.matmul(psum(buf, c, w), T.same[:], T.rel[:, BASE + col + c:BASE + col + c + w], True, True)
+                mm = PE.matmul(bank(2 * buf, c, w), T.same[:], T.rel[:, BASE + col + c:BASE + col + c + w],
+                               True, True)
             wait(q, done("p", mm))
-            freed[buf] = ends[q] = carry(q, T.tab[:, col:col + n], psum(buf, 0, n))
+            freed[buf] = carry(q, T.tab[:, col:col + n], bank(2 * buf, 0, n))
             col += n
-        ends = list(ends.values())
-        wait("s", *ends)
-        SY.dma_start(T.snap[:, 64 * (t - 1):64 * t], T.tab[0:1, 0:S]).then_inc(sem.snp, 16)
-        return ends
+        assert col == S
+        wait("p", side, *ready)
+        wait("s", *freed.values())
+        SY.dma_start(T.snap[:, t - 1, :], T.tab[0:1, 0:S]).then_inc(sem.snp, 16)
+        return freed
 
-    def peel(t, ends):
-        for q in "vap":
-            wait(q, *ends)
-        plan = {q: [k for k in ORDER[q] if t == R or k[0] not in "wWc"] for q in ORDER}
-        xs = [psum(j // 2, 512 * (j % 2), 16 * (c1 - c0)) for j, (c0, c1) in enumerate(CHUNKS)]
-
-        def zpart(j, k0, k1):
-            return ps[2 + j // 2][:, 8 * (j % 2) + k0:8 * (j % 2) + k1, 0:CHUNKS[j][1] - CHUNKS[j][0]]
-
-        for j, (c0, c1) in enumerate(CHUNKS):
-            PE.matmul(zpart(j, 0, 4), T.eye[:], T.hi[:, :, c0:c1], True, False)
-            PE.matmul(zpart(j, 0, 4), T.eye[:], T.lo[:, :, c0:c1], False, False)
-            PE.matmul(xs[j], T.eye[:], T.pk[:, 16 * c0:16 * c1], True, False)
+    def peel(t, freed):
+        for q in "va":
+            wait(q, *freed.values())
+        wait("p", c_wrap, i_slot if t == 2 else i_all)
+        plan = {q: tasks(ORDER[t][q]) for q in "vap"}
+        every = plan["v"] + plan["a"] + plan["p"]
+        banks = [2 * buf + h for buf in freed for h in range(2)]
+        home = {k: banks[i] for i, k in enumerate(k for k in plan["p"] if k[0] in "BKD")}
+        pk, look, wide = (T.pk, T.look, 64) if t <= 3 else (T.pk2, T.look2, LEFT)
         mark, scats = {}, []
-        lists = [k for q in "va" for k in ORDER[q] if k[0] == "g"]
+
+        def meet(kinds, k, back=0):
+            return [d for d in every if d[0] in kinds and d[1] < k[2] and k[1] - back < d[2]
+                    and (k[0] + d[0] != "Xg" or k[3] == d[3]) and d != k]
 
         def needs(q, k):
-            j = k[1]
-            if k[0] in "gw":
-                return []
-            if k[0] == "X":
-                return [d for d in lists if d[1] == j and d[2] < 2 * k[2] + 2 and d[3] > 2 * k[2]]
-            if k[0] in "ZD":
-                return [d for d in lists if d[1] == j]
-            return {"u": [("X", j, d) for d in range(4)], "U": [("u", j)], "n": [("r", j, d) for d in range(4)],
-                    "r": [("Z", j)], "o": [("n", j)], "y": [("U" if q == "a" else "u", j)],
-                    "s": [("y", j), ("o", j)], "W": [("w", j)], "c": [("W", j)]}[k[0]]
+            before = {"X": "g", "Z": "g", "D": "g", "r": "Z", "n": "r", "o": "n", "u": "X", "U": "u", "s": "yo",
+                      "y": "U" if q == "a" else "u", "W": "r", "c": "W", "m": "X", "f": "n", "j": "q",
+                      "C": "E"}
+            if t == 3:
+                before.update(u="m", o="j")
+            if k[0] in "Pq":
+                return meet("f", k, 1) if k[0] == "P" else meet("P", k) + [d for d in meet("q", k, 1) if d < k]
+            return meet(before.get(k[0], ""), k)
 
         def emit(q, k):
-            j = k[1]
-            c0, c1 = CHUNKS[j]
+            kind, c0, c1, place = k
             n = c1 - c0
-            x, u, val = xs[j], T.u[:, 16 * c0:16 * c1], T.val[:, 16 * c0:16 * c1]
-            twin = psum(1, 512, 16 * n)
-
-            def place(i):
-                return T.gat[:, 64 * c0 + 16 * n * i:64 * c0 + 16 * n * (i + 1)]
-
-            if k[0] == "w":
-                wait(q, ("snp", 64))
-                return done(q, A.activation(T.sna[:], T.snap[:], Act.Relu, scale=1.0 / MARK))
-            if k[0] == "W":
-                for i in range(4):
-                    mm = PE.matmul(psum(3, 512, 64), T.eye[:], T.sna[:, 64 * i:64 * i + 64], i == 0, i == 3)
-                return done(q, mm)
-            if k[0] == "c":
-                return done(q, A.activation(T.rnd[:], psum(3, 512, 64), Act.Identity, bias=1.0))
-            if k[0] == "g":
-                a, b = 4 * c0 + k[2] * n // 2, 4 * c0 + k[3] * n // 2
-                src, dst = T.tab[:, 0:S + 1].indirect(T.look[:, a:b]), T.gat[:, 16 * a:16 * b]
+            if kind in "KXuyDUm":
+                xk = meet("D" if kind == "U" or kind + q == "ya" else "K", k)[0] if kind not in "KD" else k
+                x = bank(home[xk], 16 * (c0 - xk[1]), 16 * n)
+            if kind in "BZrWcPq":
+                zb = home[meet("B", k)[0] if kind != "B" else k]
+            u, val = T.u[:, 16 * c0:16 * c1], T.val[:, 16 * c0:16 * c1]
+            state = T.st5[:, 5 * c0 + 4:5 * c1:5]
+            if kind in "BKD":
+                wait(q, freed[home[k] // 2])
+            if kind in "KD":
+                mm = PE.matmul(x, T.eye[:], pk[:, 16 * c0:16 * c1], True, False)
+                for i in range(4 if kind == "D" else 0):
+                    mm = PE.matmul(x, T.neye[:], T.gat[:, 16 * c0:16 * c1, i], False, False)
+                return mm
+            if kind == "B":
+                PE.matmul(rows(zb, 0, n, slice(0, 5)), T.sl[0:1, :], T.sr[0:1, 5 * c0:5 * c1], True, False)
+                if t > 3:
+                    return digits(lambda b: rows(zb, b, n, slice(1, 5), 2), c0, c1, 4, False)
+                PE.matmul(rows(zb, 0, n, slice(1, 5)), T.eye[:], T.hl[:, c0:c1, :], False, False)
+                return PE.matmul(rows(zb, 0, n, slice(1, 5)), T.eye[:], T.hl[:, 64 + c0:64 + c1, :], False, False)
+            if kind == "g":
+                src = T.tab[:, 0:S + 1].indirect(look[:, wide * place + c0:wide * place + c1])
+                dst = T.gat[:, 16 * c0:16 * c1, place]
                 return done(q, V.tensor_copy(dst, src) if q == "v" else A.activation(dst, src, Act.Identity))
-            if k[0] == "X":
-                end = k == [d for d in ORDER["p"] if d[:2] == k[:2]][-1]
-                return done(q, PE.matmul(x, T.neye[:], place(k[2]), False, end))
-            if k[0] == "Z":
+            if kind == "X":
+                end = k == [d for d in plan["p"] if d in meet("X", xk)][-1]
+                return done(q, PE.matmul(x, T.neye[:], T.gat[:, 16 * c0:16 * c1, place], False, end))
+            if kind == "Z":
                 for r in range(16):
-                    mm = PE.matmul(zpart(j, 0, 4), T.wrap[:, 128 * r:128 * r + 128],
-                                   T.gat[:, 64 * c0 + r:64 * c1:16], False, r == 15)
+                    mm = PE.matmul(rows(zb, 0, n, slice(1, 5)), T.wrap[:, 128 * r:128 * r + 128],
+                                   T.gat[:, 16 * c0 + r:16 * c1:16, :], False, r == 15)
                 return done(q, mm)
-            if k[0] == "D":
-                PE.matmul(twin, T.eye[:], T.pk[:, 16 * c0:16 * c1], True, False)
-                for i in range(4):
-                    mm = PE.matmul(twin, T.neye[:], place(i), False, False)
-                return done(q, mm)
-            if k[0] == "U":
-                return done(q, PE.matmul(twin, T.neye[:], u, False, True))
-            if k[0] == "r":
-                m5, z = T.m5[:, 5 * c0 + 1 + k[2]:5 * c1:5], zpart(j, k[2], k[2] + 1)
-                return done(q, A.activation(m5, z, Act.Relu) if q == "a" else
-                            V.tensor_scalar(m5, z, 0.0, None, Op.max))
-            if k[0] == "n":
+            if kind == "U":
+                return done(q, PE.matmul(x, T.neye[:], u, False, True))
+            if kind == "r":
+                m5, z = T.m5[:, 5 * c0:5 * c1], rows(zb, 0, n, slice(0, 5))
+                less = T.pf[:, 4:5] if t <= 3 else T.pf[:, 5:6]
+                return done(q, A.activation(m5, z, Act.Relu, bias=less) if q == "a" else
+                            V.tensor_scalar(m5, z, less, 0.0, Op.add, Op.max))
+            if kind == "n":
                 return done(q, V.tensor_tensor_scan(T.st5[:, 5 * c0:5 * c1], T.m5[:, 5 * c0:5 * c1],
                                                     T.lim[:, 5 * c0:5 * c1], 0.0, Op.add, Op.min))
-            if k[0] == "o":
-                return done(q, V.tensor_copy(T.off[:, c0:c1], T.st5[:, 5 * c0 + 4:5 * c1:5]))
-            if k[0] == "u":
+            if kind == "f":
+                return done(q, A.activation(T.flag[:, 1 + c0:1 + c1], state, Act.Sign, bias=0.5 - BASE - S))
+            if kind == "P":
+                for i in range(3):
+                    at = c0 + (i == 0)
+                    mm = PE.matmul(rows(zb, 0, n, 5), T.rank[:, i, :], T.flag[:, at:at + n], i == 0, i == 2)
+                return done(q, mm)
+            if kind == "q":
+                return done(q, V.tensor_tensor_scan(T.cand[:, c0:c1], rows(zb, 0, n, 5), T.eight[:, c0:c1],
+                                                    T.cand[:, c0 - 1:c0] if c0 else KEPT + AWAY, Op.add, Op.add))
+            if kind == "j":
+                return done(q, V.tensor_tensor(T.one[:, c0:c1], state, T.cand[:, c0:c1], Op.min))
+            if kind == "o":
+                return done(q, V.tensor_copy(T.off[:, c0:c1], T.one[:, c0:c1] if t == 3 else state))
+            if kind == "E":
+                for i in range(8):
+                    part, par, b = i // 4, i // 2 % 2, i % 2
+                    mm = PE.matmul(rows(banks[7], 32 * part, 32 * part + 32, slice(4 * par, 4 * par + 4)),
+                                   hop(par, b, 0), T.hl[:, 64 * part + b:64 * part + 64:2, :], b == 0, b == 1)
+                return done(q, mm)
+            if kind == "C":
+                done(q, A.activation(T.dig[:, :, 0:8:2], bank(banks[7], 0, 256), Act.Identity, bias=CUT + 256,
+                                     scale=1.0 / 128))
+                busy[banks[7] // 2] = done(q, A.activation(T.dig[:, :, 1:8:2], bank(banks[7], 256, 256),
+                                                           Act.Identity, bias=CUT + 64))
+                return busy[banks[7] // 2]
+            if kind == "m":
+                return done(q, V.tensor_tensor(x, x, T.cut[:, 16 * c0:16 * c1], Op.min))
+            if kind == "u":
                 return done(q, A.activation(u, x, Act.Identity, bias=-127.5) if q == "a" else
                             V.tensor_scalar(u, x, -127.5, None, Op.add))
-            if k[0] == "y":
-                return done(q, A.activation(val, twin, Act.Identity) if q == "a" else
+            if kind == "y":
+                return done(q, A.activation(val, x, Act.Identity) if q == "a" else
                             V.tensor_tensor(val, x, u, Op.subtract))
+            if kind == "W":
+                wait(q, ("snp", 64))
+                for i in range(4):
+                    mm = PE.matmul(bank(zb, 0, 64), T.eye[:], T.snap[:, i, :], i == 0, i == 3)
+                return done(q, mm)
+            if kind == "c":
+                wait(q, done(q, A.activation(T.blk[:, 0:64], bank(zb, 0, 64), Act.Identity, bias=129.0,
+                                             scale=1.0 / MARK)))
+                return done(q, A.activation(T.rnd[:], T.blk[:, 0:64], Act.Identity, bias=-128.0))
             wait(q, *scats)
             scats.append(done(q, V.tensor_copy(T.rel[:, 0:WREL].indirect(T.off[:, c0:c1]), val)))
             return scats[-1]
@@ -284,45 +427,38 @@ def rank_program(g, core, T, topo):
                     wait(q, *[mark[d] for d in needs(q, k)])
                     mark[k] = emit(q, k)
                     at[q] += 1
-        return scats[-1], mark
+        return scats[-1], [mark[k] for k in every if k[0] == "c"]
 
     for t in range(1, R):
-        last, mark = peel(t + 1, spread(t, last))
+        last, rounds = peel(t + 1, spread(t, last))
 
-    wait("s", mark[("c", 0)])
-    SY.dma_start(T.stw[:], T.rnd[:]).then_inc(sem.stgw, 16)
-    SY.dma_start(T.lnw[me], T.rnd[16 * me:16 * me + 16, :]).then_inc(sem.ownw, 16)
-    wait("g", ("stgw", 16))
-    sent += send(order, [2] + [1] * 6, lambda r: T.stw[r], T.lnw[me], "arw")
-    wait("p", last, c_lay, mark[("c", 0)])
+    wait("s", *rounds)
+    stage(("w", T.rnd))
+    wait("p", last, *rounds)
     made = {}
     for b, r in enumerate(order + [me]):
-        out = psum(b // 2, 512 * (b % 2), 128)
         for a in range(8):
             col = BASE + P * r + 128 * a
-            mm = PE.matmul(out, T.lay[:, 128 * a:128 * a + 128], T.rel[:, col:col + 128], a == 0, a == 7)
+            mm = PE.matmul(rows(b, 0, 16, a), T.rel[:, col:col + 128], T.same[:, 0:16], True, True)
         q = "va"[b % 2]
         wait(q, done("p", mm))
-        made[r] = carry(q, (T.yf if r == me else T.msg)[:, 128 * r:128 * r + 128], out)
+        made[r] = carry(q, (T.land if r == me else T.msg)[:, r, :], bank(b, 0, 128))
     for first, end, width in BATCHES:
         wait("g", *[made[r] for r in order[first:end]])
-        sent += send(order[first:end], [width] * (end - first), lambda r: T.msg[:, 128 * r:128 * r + 128],
-                     T.land[:, 128 * me:128 * me + 128], "ya%d" % me)
-    stores = {"s": 0, "a": 0}
-
-    def store(q, r, made_by):
-        wait(q, made_by)
-        queue[q].dma_start(T.y[16 * r:16 * r + 16, :], T.yf[:, 128 * r:128 * r + 128]).then_inc(
-            sem.outa if q == "s" else sem.outb, 16)
-        stores[q] += 16
-
-    store("s", me, made[me])
+        sent += send(order[first:end], width, lambda r: T.msg[:, r, :], T.land[:, me, :], "ya%d" % me)
+    sent += deal("w")
+    wait("p", *made.values())
     turn = {r: peers(r, cores, topo).index(me) for r in order}
-    for i, r in enumerate(sorted(order, key=lambda r: turn[r])):
-        wait("v", ("ya%d" % r, [w for first, end, w in BATCHES if first <= turn[r] < end][0]))
-        store("as"[i % 2], r, done("v", V.tensor_copy(T.yf[:, 128 * r:128 * r + 128], T.land[:, 128 * r:128 * r + 128])))
-    wait("s", ("ownw", 16), ("arw", N - 1 + sum(1 for r in order if turn[r] == 0)))
-    SY.dma_start(T.rounds[:], T.lnw[:]).then_inc(sem.outa, 16)
-    wait("s", ("outa", stores["s"] + 16))
-    wait("a", ("outb", stores["a"]))
+    for i, r in enumerate([me] + sorted(order, key=lambda r: turn[r])):
+        if r != me:
+            wait("p", ("ya%d" % r, [w for first, end, w in BATCHES if first <= turn[r] < end][0]))
+        wait("v", done("p", PE.matmul(bank(i, 0, 128), T.land[:, r, :], T.eye[:], True, True)))
+        wide = T.yf[:, 128 * r:128 * r + 128]
+        q = "sa"[i % 2]
+        wait(q, done("v", V.tensor_copy(wide, bank(i, 0, 128))))
+        if i == N - 1:
+            load("s", "w", T.rounds[:])
+        queue[q].dma_start(T.y[16 * r:16 * r + 16, :], wide).then_inc(sem.outa if q == "s" else sem.outb, 16)
+    wait("s", ("outa", 8 * N), ("ldw", 16))
+    wait("a", ("outb", 8 * N))
     wait("g", ("sent", sent), ("v", count["v"]), ("a", count["a"]), ("p", count["p"]), ("g", count["g"]))

from concourse.bass import DstId, RemoteDMATransfer
from concourse.mybir import AluOpType as Op, ActivationFunctionType as Act

N, S, P, R = 8, 8192, 1024, 5
MARK = -49152.0
BASE = 16384
WREL = BASE + S + 1136
KEPT = 2048
LEFT = 36
FILL = 2048
BIG = 1.0e9
FAR = 1048576.0
DEG = 32768.0
CUT = 57344.0
AWAY = 32768.0

SCRATCH = {
    "pk": ("sbuf", [128, P], "bfloat16"), "nbi": ("sbuf", [128, 4, 64], "int32"),
    "rel": ("sbuf", [128, WREL], "bfloat16"), "tab": ("sbuf", [128, S + 16], "bfloat16"),
    "gat": ("sbuf", [128, P, 4], "bfloat16"),
    "sum2": ("sbuf", [128, 128], "float32"), "sum1": ("sbuf", [128, 64], "float32"),
    "one": ("sbuf", [128, 64], "float32"), "top": ("sbuf", [128, 64], "float32"),
    "off": ("sbuf", [128, 64], "uint16"), "look": ("sbuf", [128, 256], "uint16"),
    "hl": ("sbuf", [128, 128, 4], "bfloat16"),
    "m5": ("sbuf", [128, 320], "float32"), "lim": ("sbuf", [128, 320], "float32"),
    "st5": ("sbuf", [128, 320], "float32"), "slot": ("sbuf", [128, 64], "float32"),
    "u": ("sbuf", [128, P], "bfloat16"), "val": ("sbuf", [128, P], "bfloat16"),
    "jw": ("sbuf", [128, 160], "int32"), "jb": ("sbuf", [128, 128], "int32"),
    "eyew": ("sbuf", [128, 160], "bfloat16"), "eye": ("sbuf", [128, 128], "bfloat16"),
    "neye": ("sbuf", [128, 128], "bfloat16"),
    "same": ("sbuf", [128, 128], "bfloat16"), "samef": ("sbuf", [128, 16], "float32"),
    "wrap": ("sbuf", [128, 16 * 128], "bfloat16"),
    "sl": ("sbuf", [128, 128], "bfloat16"), "sr": ("sbuf", [128, 320], "bfloat16"),
    "pi": ("sbuf", [128, 2], "int32"), "pf": ("sbuf", [128, 6], "float32"), "blk": ("sbuf", [128, 128], "bfloat16"),
    "rank": ("sbuf", [128, 3, 128], "bfloat16"), "hop": ("sbuf", [128, 4, 160], "bfloat16"),
    "dig": ("sbuf", [128, 64, 16], "float32"), "nbf": ("sbuf", [128, 4, 64], "float32"),
    "eyef": ("sbuf", [128, 128], "float32"),
    "cut": ("sbuf", [128, P], "float32"),
    "flag": ("sbuf", [128, 66], "bfloat16"), "eight": ("sbuf", [128, 64], "float32"),
    "cand": ("sbuf", [128, 64], "float32"), "kept": ("sbuf", [128, LEFT // 2, 32], "bfloat16"),
    "look2": ("sbuf", [128, 5 * LEFT], "uint16"), "pk2": ("sbuf", [128, 16 * LEFT], "bfloat16"),
    "snap": ("sbuf", [128, 4, 64], "bfloat16"), "rnd": ("sbuf", [128, 64], "float32"),
    "msg": ("sbuf", [128, N, 128], "bfloat16"), "land": ("sbuf", [128, N, 128], "bfloat16"),
    "yf": ("sbuf", [128, P], "float32"),
    "ps0": ("psum", [128, 128, 8], "float32"), "ps1": ("psum", [128, 128, 8], "float32"),
    "ps2": ("psum", [128, 128, 8], "float32"), "ps3": ("psum", [128, 128, 8], "float32"),
}
PARTS = {"n": ("int32", 32), "p": ("bfloat16", 128), "w": ("float32", 8)}
for _k, (_d, _w) in PARTS.items():
    SCRATCH["st_" + _k] = ("dram", [N, 128, _w], _d)
    SCRATCH["ln_" + _k] = ("dram", [N, 128, _w], _d)
SEMAPHORES = (["cv", "ca", "cp", "cg", "sent", "snp", "outa", "outb"] + ["ya%d" % i for i in range(N)]
              + [a + k for k in PARTS for a in ("stg", "arr", "ld")])

ORDER = {
    2: {"v": "g0-20.2 g0-20.1 g20-48.2 g20-48.1 r0-20 u0-20 g48-64.0 n0-20 y0-20 o0-20 s0-20 n20-48 y20-48 "
             "o20-48 n48-64 s20-48 o48-64 s48-64",
        "a": "g0-20.0 g0-20.3 g20-48.0 g20-48.3 g48-64.3 g48-64.1 g48-64.2 r20-48 u20-48 r48-64 u48-64 y48-64 "
             "C0-64",
        "p": "K0-20 B0-20 B20-48 K20-48 B48-64 K48-64 X0-20.2 X0-20.0 Z0-20 X0-20.3 X0-20.1 X20-48.0 X20-48.2 "
             "Z20-48 X20-48.3 X20-48.1 X48-64.3 Z48-64 X48-64.1 X48-64.0 X48-64.2 D48-64 U48-64 E0-64"},
    3: {"v": "g0-18.1 g0-18.0 g18-44.2 g18-44.1 r0-18 n0-18 m0-18 u0-18 y0-18 q0-18 j0-18 m18-44 o0-18 s0-18 "
             "n18-44 r44-64 n44-64 y18-44 m44-64 q18-44 j18-44 q44-64 o18-44 j44-64 s18-44 o44-64 y44-64 s44-64",
        "a": "g0-18.3 g0-18.2 g18-44.3 g18-44.0 g44-64.1 f0-18 g44-64.3 g44-64.0 g44-64.2 r18-44 u18-44 f18-44 "
             "f44-64 u44-64",
        "p": "K0-18 B0-18 K18-44 B18-44 B44-64 K44-64 X0-18.1 X0-18.3 Z0-18 X0-18.0 X0-18.2 X18-44.2 X18-44.3 "
             "X18-44.1 P0-18 X18-44.0 Z18-44 Z44-64 X44-64.2 X44-64.3 X44-64.1 X44-64.0 P18-44 P44-64"},
    4: {"v": "g0-16.0 g0-16.1 g16-36.1 g16-36.0 r0-16 n0-16 o0-16 y0-16 s0-16 y16-36 n16-36 o16-36 s16-36",
        "a": "g0-16.2 g0-16.3 g16-36.2 g16-36.3 u0-16 u16-36 r16-36",
        "p": "K0-16 B0-16 K16-36 B16-36 X0-16.2 X0-16.0 X0-16.1 X0-16.3 Z0-16 X16-36.2 X16-36.1 X16-36.3 "
             "X16-36.0 Z16-36"},
}
ORDER[5] = {"v": ORDER[4]["v"], "a": ORDER[4]["a"] + " c0-16", "p": ORDER[4]["p"] + " W0-16"}
PIECES = {
    1: "a512 v704 a672 v768 a896 v960 a992 v960 a1024 v704",
    2: "a576 R v480 a832 v928 a864 v960 a960 v896 a1024 v672",
    3: "T a512 v256 E a320 L v480 G v928 a960 v864 a512 v960 a960 v928 a512",
    4: "v448 a512 v640 a672 v704 a576 v832 a736 v928 a768 v800 a576",
}
BATCHES = [(0, 2, 4), (2, 6, 2), (6, 7, 8)]


def tasks(text):
    return [(w[0],) + tuple(int(n) for n in (w[1:] + ".0").replace("-", ".").split(".")[:3]) for w in text.split()]


def peers(src, cores, topo):
    def far(r):
        a, b = topo.chip(cores[src]), topo.chip(cores[r])
        return 2 if topo.mates(a, b) else (1 if topo.same_plane(a, b) else 0)
    return sorted([r for r in range(N) if r != src], key=lambda r: (far(r), (r - src) % N))


def rank_program(g, core, T, topo):
    me = T.rank_of(core)
    if me is None:
        return
    cores = list(T.cores)
    sem = T.sem
    V, A, PE, SY = g.vector, g.scalar, g.tensor, g.sync
    queue = {"v": V, "a": A, "p": PE, "s": SY, "g": g}
    count = {"v": 0, "a": 0, "p": 0, "g": 0}
    seen = {}

    def done(q, ins):
        ins.then_inc(sem["c" + q], 1)
        count[q] += 1
        return (q, count[q])

    def wait(q, *marks):
        for src, n in marks:
            name = "c" + src if src in count else src
            if seen.get((q, name), 0) < n:
                queue[q].wait_ge(sem[name], n)
                seen[(q, name)] = n

    def step(ins, *marks):
        wait("v", ("v", count["v"]), *marks)
        return done("v", ins())

    def iota(out, pattern, base, by):
        if count["g"] >= 3:
            wait("g", ("g", count["g"]))
        return done("g", g.iota(out, pattern, base, by, allow_small_or_imprecise_dtypes=True))

    order = peers(me, cores, topo)

    def send(dsts, width, src_of, dst_ap, sem_name):
        tr = []
        for i, r in enumerate(dsts):
            rid, pid, _ = topo.addr(cores[r])
            mask = sum(1 << e for e in topo.engines(core, cores[r])[i * width:(i + 1) * width])
            tr.append(RemoteDMATransfer(dst_ids=[DstId(rid=rid, pnc=pid)], dma_engine_mask=mask,
                                        remote_sem=sem[sem_name], src=src_of(r), dst=dst_ap))
        g.remote_dma_fused(tr, local_sem=sem.sent)
        return width * len(dsts)

    ps = [T.ps0, T.ps1, T.ps2, T.ps3]

    def rows(b, first, end, cols, by=1):
        return ps[b // 2][:, 64 * (b % 2) + first:64 * (b % 2) + end:by, cols]

    def bank(b, col, n):
        return rows(b, col // 8, (col + n) // 8, slice(0, 8))

    def stage(*parts):
        for k, src in parts:
            SY.dma_start(T["st_" + k][:], src[:]).then_inc(sem["stg" + k], 16)
        for k, src in parts:
            SY.dma_start(T["ln_" + k][me], src[16 * me:16 * me + 16, :]).then_inc(sem["arr" + k], 16)

    def deal(k):
        wait("g", ("stg" + k, 16))
        return send(order, 1, lambda r: T["st_" + k][r], T["ln_" + k][me], "arr" + k)

    def load(q, k, dst):
        wait(q, ("arr" + k, 16 + N - 1))
        queue[q].dma_start(dst, T["ln_" + k][:]).then_inc(sem["ld" + k], 16)

    stage(("n", T.nb), ("p", T.packets))
    iota(T.jw[:], [[1, 160]], 1008, -1)
    iota(T.slot[:], [[16, 64]], 0, 1)
    i_a = iota(T.pi[:, 0:1], [[0, 1]], 0, 1)
    sent = deal("n") + deal("p")
    load("s", "n", T.nbi[:])
    load("s", "p", T.pk[:])

    ja = T.jw[:, 16:144]
    wait("a", done("v", V.memset(T.rel[:, BASE:BASE + FILL], MARK)))
    m_fill = done("a", A.activation(T.rel[:, BASE + FILL:BASE + 2 * FILL], T.rel[:, BASE:BASE + FILL], Act.Identity))
    for ap, value in ((T.lim[:], BIG), (T.sl[0:1, :], 1.0), (T.dig[:, :, 10:16], CUT), (T.eight[:], 8.0),
                      (T.flag[:], -1.0), (T.tab[:, S:S + 16], 0.0), (T.rel[:, KEPT:KEPT + 16 * LEFT], 64.0),
                      (T.blk[:], 0.5), (T.rank[:, 2, :], AWAY / 2)):
        m = done("v", V.memset(ap, value))
    wait("g", m)
    iota(T.sr[0:1, :], [[-16, 64], [0, 5]], 0, 0)
    iota(T.sr[0:1, 0::5], [[0, 64]], int(FAR), 0)
    iota(T.pf[:, 4:5], [[0, 1]], 0, -1)
    i_slot = iota(T.pf[:, 5:6], [[0, 1]], BASE + int(MARK) - 64, -1)
    iota(T.dig[:, :, 8], [[1, 8], [0, 8]], int(CUT) + 64, 0)
    for first in range(0, 128, 32):
        i_dig = iota(T.dig[first:first + 32, :, 9], [[0, 8], [32, 4], [0, 2]], int(CUT) + 64, 1)
    for out, of, pattern, test, fill, base, by in (
            (T.blk[:], T.blk[:], [[-16, 8], [0, 16]], Op.is_ge, 0.0, 0, 1),
            (T.blk[:], T.blk[:], [[16, 8], [0, 16]], Op.is_ge, 0.0, 15, -1),
            (T.rank[:, 0, :], T.blk[:], [[1, 128]], Op.is_gt, 0.0, 0, -1),
            (T.rank[:, 0, :], T.rank[:, 0, :], [[1, 128]], Op.not_equal, -AWAY / 2, 0, -1),
            (T.rank[:, 1, :], T.blk[:], [[-1, 128]], Op.is_ge, 0.0, 0, 1),
            (T.rank[:, 2, :], T.rank[:, 2, :], [[1, 128]], Op.is_equal, 0.0, 0, -1)):
        wait("g", ("g", count["g"]))
        i_all = done("g", g.affine_select(out, of, pattern, test, fill, base, by))
    step(lambda: V.tensor_scalar(T.eyew[:], T.jw[:], 1024.0, None, Op.is_equal), i_a)
    done("v", V.tensor_scalar(T.jb[:], ja, 15, None, Op.bitwise_and))
    done("v", V.tensor_scalar(T.pi[:, 1:2], T.pi[:, 0:1], 4, 1, Op.arith_shift_right, Op.bitwise_and))
    step(lambda: V.tensor_scalar(T.samef[:], T.jb[:, 0:16], 0.0, -1.0, Op.is_equal, Op.mult))
    for i in range(4):
        m = done("v", V.tensor_scalar(T.pf[:, i:i + 1], T.pi[:, 1:2], float(i % 2), 128.0 ** (i // 2),
                                      Op.is_equal, Op.mult))
    wait("a", m)
    made = [(T.hop[:, i, :], T.eyew[:], T.pf[:, i:i + 1], 0.0) for i in range(4)]
    made += [(T.eye[:], T.eyew[:, 16:144], 1.0, 0.0), (T.eyef[:], T.eyew[:, 16:144], 1.0, 0.0),
             (T.neye[:], T.eyew[:, 16:144], -1.0, 0.0),
             (T.lim[:, 0::5], T.slot[:], 1.0, 0.0), (T.lim[:, 4::5], T.slot[:], 1.0, float(BASE + S))]
    for out, of, scale, bias in made:
        c_hop = done("a", A.activation(out, of, Act.Identity, bias=bias, scale=scale))
    for r in range(16):
        c_wrap = done("a", A.activation(T.wrap[:, 128 * r:128 * r + 128], T.eyew[:, 16:144], Act.Identity,
                                        scale=T.samef[:, r:r + 1]))
    done("v", V.tensor_scalar(T.same[:], T.jb[:], 0.0, None, Op.is_equal))
    done("v", V.tensor_scalar(T.top[:], T.slot[:], 4.0 * S + DEG, None, Op.add))
    done("v", V.memset(T.rel[:, BASE + 2 * FILL:BASE + S], MARK))

    def hop(b, to, big):
        return T.hop[:, 2 * big + b, 16 - 16 * (to - b):144 - 16 * (to - b)]

    step(lambda: V.tensor_scalar(bank(0, 0, 256), T.nbi[:], float(S), DEG, Op.is_lt, Op.mult), ("ldn", 16))
    step(lambda: V.tensor_tensor(T.sum2[:], bank(0, 0, 128), T.nbi[:, 0:2, :], Op.add))
    done("v", V.tensor_tensor(bank(1, 0, 128), bank(0, 128, 128), T.nbi[:, 2:4, :], Op.add))
    step(lambda: V.tensor_tensor(T.sum1[:], bank(1, 0, 64), T.sum2[:, 0:64], Op.add))
    done("v", V.tensor_tensor(bank(0, 0, 64), bank(1, 64, 64), T.sum2[:, 64:128], Op.add))
    step(lambda: V.tensor_tensor(bank(1, 0, 64), bank(0, 0, 64), T.sum1[:], Op.add))
    step(lambda: V.tensor_tensor(T.one[:], bank(1, 0, 64), T.top[:], Op.min))
    m_off = step(lambda: V.tensor_scalar(T.off[:], T.one[:], BASE - 3.0 * S - DEG, None, Op.add))
    m = done("v", V.tensor_copy(T.nbf[:], T.nbi[:]))
    wait("v", m_off, m_fill, ("ldp", 16))
    last = done("v", V.tensor_copy(T.rel[:, 0:WREL].indirect(T.off[:]), T.pk[:]))
    done("v", V.tensor_copy(T.look[:], T.nbi[:]))
    wait("p", m, c_hop)
    for part in range(2):
        if part:
            wait("p", m_parts)
            PE.matmul(rows(7, 0, 64, slice(0, 4)), T.neye[:], T.hl[:, 0:64, :], True, False)
        for k in range(4):
            mm = PE.matmul(rows(6 + part, 0, 64, k), T.eyef[:], T.nbf[:, k, :], not part, not part or k == 3)
        wait("a", done("p", mm))
        m_parts = done("a", A.activation(T.hl[:, 64 * part:64 * part + 64, :], rows(6 + part, 0, 64, slice(0, 4)),
                                         Act.Identity, bias=BASE + MARK))

    def carry(q, dst, src):
        if q == "v":
            return done("v", V.tensor_scalar(dst, src, -7 * MARK, None, Op.add))
        return done("a", A.activation(dst, src, Act.Identity, bias=-7 * MARK))

    ready, busy = [], {3: m_parts}

    def lists(kind, before):
        if kind == "R":
            wait("v", i_dig, *busy.values())
            return done("v", V.transpose(T.cut[:], T.dig[:]))
        if kind == "T":
            wait("v", before)
            return done("v", V.transpose(T.kept[:], T.rel[:, KEPT:KEPT + 16 * LEFT]))
        if kind == "E":
            wait("p", before)
            return done("p", digits(lambda b: rows(7, b, LEFT, slice(0, 5), 2), 0, LEFT, 5, True))
        if kind == "L":
            wait("v", before)
            for k in (4, 0, 1, 2, 3):
                m = done("v", V.tensor_scalar(T.look2[:, LEFT * k:LEFT * k + LEFT], rows(7, 0, LEFT, k),
                                              -64.0 * (129 if k == 4 else 1), None, Op.add))
                if k == 4:
                    numbers = m
            ready.append(m)
            return numbers
        wait("a", before)
        return done("a", A.activation(T.pk2[:], T.pk[:, 0:P].indirect(T.look2[:, 4 * LEFT:5 * LEFT]), Act.Identity))

    def digits(out, c0, c1, n, alone):
        for b in range(2):
            for i in range(4):
                par, low = i // 2, i % 2
                mm = PE.matmul(out(b), hop(b, par, 1 - low),
                               T.kept[:, c0 // 2:c1 // 2, 16 * par + low:16 * par + 2 * n:2],
                               alone and i == 0, alone and i == 3)
        return mm

    def spread(t, scat):
        wait("p", scat)
        if t > 1:
            wait("v", ("snp", 16 * (t - 1)))
            wait("a", ("snp", 16 * (t - 1)))
        freed, col, turn, side = dict(busy), 0, {"v": 0, "a": 0}, scat
        for piece in PIECES[t].split():
            if len(piece) == 1:
                side = lists(piece, side)
                continue
            q, n = piece[0], int(piece[1:])
            buf = 2 * "va".index(q) + turn[q] % 2
            turn[q] += 1
            if buf in freed:
                wait("p", freed.pop(buf))
            for c in range(0, n, 512):
                w = min(512, n - c)
                mm = PE.matmul(bank(2 * buf, c, w), T.same[:], T.rel[:, BASE + col + c:BASE + col + c + w],
                               True, True)
            wait(q, done("p", mm))
            freed[buf] = carry(q, T.tab[:, col:col + n], bank(2 * buf, 0, n))
            col += n
        assert col == S
        wait("p", side, *ready)
        wait("s", *freed.values())
        SY.dma_start(T.snap[:, t - 1, :], T.tab[0:1, 0:S]).then_inc(sem.snp, 16)
        return freed

    def peel(t, freed):
        for q in "va":
            wait(q, *freed.values())
        wait("p", c_wrap, i_slot if t == 2 else i_all)
        plan = {q: tasks(ORDER[t][q]) for q in "vap"}
        every = plan["v"] + plan["a"] + plan["p"]
        banks = [2 * buf + h for buf in freed for h in range(2)]
        home = {k: banks[i] for i, k in enumerate(k for k in plan["p"] if k[0] in "BKD")}
        pk, look, wide = (T.pk, T.look, 64) if t <= 3 else (T.pk2, T.look2, LEFT)
        mark, scats = {}, []

        def meet(kinds, k, back=0):
            return [d for d in every if d[0] in kinds and d[1] < k[2] and k[1] - back < d[2]
                    and (k[0] + d[0] != "Xg" or k[3] == d[3]) and d != k]

        def needs(q, k):
            before = {"X": "g", "Z": "g", "D": "g", "r": "Z", "n": "r", "o": "n", "u": "X", "U": "u", "s": "yo",
                      "y": "U" if q == "a" else "u", "W": "r", "c": "W", "m": "X", "f": "n", "j": "q",
                      "C": "E"}
            if t == 3:
                before.update(u="m", o="j")
            if k[0] in "Pq":
                return meet("f", k, 1) if k[0] == "P" else meet("P", k) + [d for d in meet("q", k, 1) if d < k]
            return meet(before.get(k[0], ""), k)

        def emit(q, k):
            kind, c0, c1, place = k
            n = c1 - c0
            if kind in "KXuyDUm":
                xk = meet("D" if kind == "U" or kind + q == "ya" else "K", k)[0] if kind not in "KD" else k
                x = bank(home[xk], 16 * (c0 - xk[1]), 16 * n)
            if kind in "BZrWcPq":
                zb = home[meet("B", k)[0] if kind != "B" else k]
            u, val = T.u[:, 16 * c0:16 * c1], T.val[:, 16 * c0:16 * c1]
            state = T.st5[:, 5 * c0 + 4:5 * c1:5]
            if kind in "BKD":
                wait(q, freed[home[k] // 2])
            if kind in "KD":
                mm = PE.matmul(x, T.eye[:], pk[:, 16 * c0:16 * c1], True, False)
                for i in range(4 if kind == "D" else 0):
                    mm = PE.matmul(x, T.neye[:], T.gat[:, 16 * c0:16 * c1, i], False, False)
                return mm
            if kind == "B":
                PE.matmul(rows(zb, 0, n, slice(0, 5)), T.sl[0:1, :], T.sr[0:1, 5 * c0:5 * c1], True, False)
                if t > 3:
                    return digits(lambda b: rows(zb, b, n, slice(1, 5), 2), c0, c1, 4, False)
                PE.matmul(rows(zb, 0, n, slice(1, 5)), T.eye[:], T.hl[:, c0:c1, :], False, False)
                return PE.matmul(rows(zb, 0, n, slice(1, 5)), T.eye[:], T.hl[:, 64 + c0:64 + c1, :], False, False)
            if kind == "g":
                src = T.tab[:, 0:S + 1].indirect(look[:, wide * place + c0:wide * place + c1])
                dst = T.gat[:, 16 * c0:16 * c1, place]
                return done(q, V.tensor_copy(dst, src) if q == "v" else A.activation(dst, src, Act.Identity))
            if kind == "X":
                end = k == [d for d in plan["p"] if d in meet("X", xk)][-1]
                return done(q, PE.matmul(x, T.neye[:], T.gat[:, 16 * c0:16 * c1, place], False, end))
            if kind == "Z":
                for r in range(16):
                    mm = PE.matmul(rows(zb, 0, n, slice(1, 5)), T.wrap[:, 128 * r:128 * r + 128],
                                   T.gat[:, 16 * c0 + r:16 * c1:16, :], False, r == 15)
                return done(q, mm)
            if kind == "U":
                return done(q, PE.matmul(x, T.neye[:], u, False, True))
            if kind == "r":
                m5, z = T.m5[:, 5 * c0:5 * c1], rows(zb, 0, n, slice(0, 5))
                less = T.pf[:, 4:5] if t <= 3 else T.pf[:, 5:6]
                return done(q, A.activation(m5, z, Act.Relu, bias=less) if q == "a" else
                            V.tensor_scalar(m5, z, less, 0.0, Op.add, Op.max))
            if kind == "n":
                return done(q, V.tensor_tensor_scan(T.st5[:, 5 * c0:5 * c1], T.m5[:, 5 * c0:5 * c1],
                                                    T.lim[:, 5 * c0:5 * c1], 0.0, Op.add, Op.min))
            if kind == "f":
                return done(q, A.activation(T.flag[:, 1 + c0:1 + c1], state, Act.Sign, bias=0.5 - BASE - S))
            if kind == "P":
                for i in range(3):
                    at = c0 + (i == 0)
                    mm = PE.matmul(rows(zb, 0, n, 5), T.rank[:, i, :], T.flag[:, at:at + n], i == 0, i == 2)
                return done(q, mm)
            if kind == "q":
                return done(q, V.tensor_tensor_scan(T.cand[:, c0:c1], rows(zb, 0, n, 5), T.eight[:, c0:c1],
                                                    T.cand[:, c0 - 1:c0] if c0 else KEPT + AWAY, Op.add, Op.add))
            if kind == "j":
                return done(q, V.tensor_tensor(T.one[:, c0:c1], state, T.cand[:, c0:c1], Op.min))
            if kind == "o":
                return done(q, V.tensor_copy(T.off[:, c0:c1], T.one[:, c0:c1] if t == 3 else state))
            if kind == "E":
                for i in range(8):
                    part, par, b = i // 4, i // 2 % 2, i % 2
                    mm = PE.matmul(rows(banks[7], 32 * part, 32 * part + 32, slice(4 * par, 4 * par + 4)),
                                   hop(par, b, 0), T.hl[:, 64 * part + b:64 * part + 64:2, :], b == 0, b == 1)
                return done(q, mm)
            if kind == "C":
                done(q, A.activation(T.dig[:, :, 0:8:2], bank(banks[7], 0, 256), Act.Identity, bias=CUT + 256,
                                     scale=1.0 / 128))
                busy[banks[7] // 2] = done(q, A.activation(T.dig[:, :, 1:8:2], bank(banks[7], 256, 256),
                                                           Act.Identity, bias=CUT + 64))
                return busy[banks[7] // 2]
            if kind == "m":
                return done(q, V.tensor_tensor(x, x, T.cut[:, 16 * c0:16 * c1], Op.min))
            if kind == "u":
                return done(q, A.activation(u, x, Act.Identity, bias=-127.5) if q == "a" else
                            V.tensor_scalar(u, x, -127.5, None, Op.add))
            if kind == "y":
                return done(q, A.activation(val, x, Act.Identity) if q == "a" else
                            V.tensor_tensor(val, x, u, Op.subtract))
            if kind == "W":
                wait(q, ("snp", 64))
                for i in range(4):
                    mm = PE.matmul(bank(zb, 0, 64), T.eye[:], T.snap[:, i, :], i == 0, i == 3)
                return done(q, mm)
            if kind == "c":
                wait(q, done(q, A.activation(T.blk[:, 0:64], bank(zb, 0, 64), Act.Identity, bias=129.0,
                                             scale=1.0 / MARK)))
                return done(q, A.activation(T.rnd[:], T.blk[:, 0:64], Act.Identity, bias=-128.0))
            wait(q, *scats)
            scats.append(done(q, V.tensor_copy(T.rel[:, 0:WREL].indirect(T.off[:, c0:c1]), val)))
            return scats[-1]

        at = {"v": 0, "a": 0, "p": 0}
        while any(at[q] < len(plan[q]) for q in at):
            for q in at:
                while at[q] < len(plan[q]) and all(d in mark for d in needs(q, plan[q][at[q]])):
                    k = plan[q][at[q]]
                    wait(q, *[mark[d] for d in needs(q, k)])
                    mark[k] = emit(q, k)
                    at[q] += 1
        return scats[-1], [mark[k] for k in every if k[0] == "c"]

    for t in range(1, R):
        last, rounds = peel(t + 1, spread(t, last))

    wait("s", *rounds)
    stage(("w", T.rnd))
    wait("p", last, *rounds)
    made = {}
    for b, r in enumerate(order + [me]):
        for a in range(8):
            col = BASE + P * r + 128 * a
            mm = PE.matmul(rows(b, 0, 16, a), T.rel[:, col:col + 128], T.same[:, 0:16], True, True)
        q = "va"[b % 2]
        wait(q, done("p", mm))
        made[r] = carry(q, (T.land if r == me else T.msg)[:, r, :], bank(b, 0, 128))
    for first, end, width in BATCHES:
        wait("g", *[made[r] for r in order[first:end]])
        sent += send(order[first:end], width, lambda r: T.msg[:, r, :], T.land[:, me, :], "ya%d" % me)
    sent += deal("w")
    wait("p", *made.values())
    turn = {r: peers(r, cores, topo).index(me) for r in order}
    for i, r in enumerate([me] + sorted(order, key=lambda r: turn[r])):
        if r != me:
            wait("p", ("ya%d" % r, [w for first, end, w in BATCHES if first <= turn[r] < end][0]))
        wait("v", done("p", PE.matmul(bank(i, 0, 128), T.land[:, r, :], T.eye[:], True, True)))
        wide = T.yf[:, 128 * r:128 * r + 128]
        q = "sa"[i % 2]
        wait(q, done("v", V.tensor_copy(wide, bank(i, 0, 128))))
        if i == N - 1:
            load("s", "w", T.rounds[:])
        queue[q].dma_start(T.y[16 * r:16 * r + 16, :], wide).then_inc(sem.outa if q == "s" else sem.outb, 16)
    wait("s", ("outa", 8 * N), ("ldw", 16))
    wait("a", ("outb", 8 * N))
    wait("g", ("sent", sent), ("v", count["v"]), ("a", count["a"]), ("p", count["p"]), ("g", count["g"]))
